import numpy as np, ml_dtypes
CORES = [129,145,193,257,273,321,385,401,449]
N = 9
TK = 512
def setup_inputs(rng):
    return {"b": rng.standard_normal((N, 128, TK), dtype=np.float32).astype(ml_dtypes.bfloat16), "l": (rng.standard_normal((N, 128, N * 128), dtype=np.float32) / 16).astype(ml_dtypes.bfloat16)}
def setup_inputs_big(rng):
    d = setup_inputs(rng)
    for k in ("b",): d[k] = (d[k].astype(np.float32) * 1048576.0).astype(d[k].dtype)
    return d
def setup_inputs_small(rng):
    d = setup_inputs(rng)
    for k in ("b",): d[k] = (d[k].astype(np.float32) * (1 / 1048576.0)).astype(d[k].dtype)
    return d
def setup_inputs_apart(rng):
    d = setup_inputs(rng)
    f = (10.0 ** rng.permutation(np.linspace(-1.5, 1.5, N))).astype(np.float32).reshape(N, 1, 1)
    for k in ("b",): d[k] = (d[k].astype(np.float32) * f).astype(d[k].dtype)
    return d
def reference(b, l):
    B, L = b.astype(np.float64), l.astype(np.float64)
    y = np.zeros((N, 128, TK))
    for r in range(N):
        acc = B[r].copy()
        for s in range(r):
            acc -= L[s][:, 128 * r:128 * r + 128].T @ y[s]
        y[r] = acc
    return {"y": y.astype(ml_dtypes.bfloat16)}

@@ -1,0 +1,185 @@
+from concourse.bass import DstId, RemoteDMATransfer
+from concourse.mybir import AluOpType
+
+N, P, TK = 9, 128, 512
+K = 2
+W = TK // K
+R1 = 4
+
+
+def _ns(s):
+    return (R1 - s) if s < R1 else (N - 1 - s)
+
+
+def _nl(s):
+    return (N - 1 - R1) if s < R1 else 0
+
+
+_OFF1, _OFF2, _c = [], [], 0
+for _s in range(N):
+    _OFF1.append(_c)
+    _c += W + P * _ns(_s)
+for _s in range(N):
+    _OFF2.append(_c)
+    _c += P * _nl(_s)
+
+SCRATCH = {
+    "stage": ("sbuf", [P, 2 * W + P * (N - 1)], "bfloat16"),
+    "land": ("sbuf", [P, _c], "bfloat16"),
+    "ys": ("sbuf", [P, (N - 1) * W], "bfloat16"),
+    "yl": ("sbuf", [P, TK], "bfloat16"),
+}
+for _r in range(1, N):
+    SCRATCH["ps%d" % _r] = ("psum", [P, 512], "float32")
+
+SEMAPHORES = (["ldE", "ldL", "sent", "res0", "res1", "st0", "st1"]
+              + ["inE%d" % s for s in range(N)] + ["inL%d" % s for s in range(R1)]
+              + ["mm%d" % r for r in range(1, N)] + ["yv%d" % r for r in range(1, N)])
+
+
+def _bits(mask):
+    return [1 << i for i in range(mask.bit_length()) if (mask >> i) & 1]
+
+
+def _split(mask, parts):
+    e = _bits(mask)
+    n = len(e) // parts
+    return [sum(e[i * n:(i + 1) * n]) for i in range(parts)]
+
+
+def rank_program(g, core, T, topo):
+    rank = T.rank_of(core)
+    if rank is None:
+        return
+    cores = list(T.cores)
+    hubs = [c for c in cores
+            if all(topo.may_write(c, d) and topo.may_write(d, c) for d in cores if d != c)]
+    solvers = hubs[:K]
+    me_k = solvers.index(core) if core in solvers else None
+    sem = T.sem
+    s = rank
+    ns, nl = _ns(s), _nl(s)
+    late0 = 2 * W + P * ns
+
+    nE = 32
+    g.sync.dma_start(T.stage[:, 0:W], T.b[:, 0:W]).then_inc(sem.ldE, 16)
+    if ns:
+        g.scalar.dma_start(T.stage[:, W:W + P * ns], T.l[:, P * (s + 1):P * (s + 1 + ns)]).then_inc(sem.ldE, 16)
+        nE += 16
+    g.sync.dma_start(T.stage[:, W + P * ns:late0], T.b[:, W:TK]).then_inc(sem.ldE, 16)
+    if nl:
+        g.scalar.dma_start(T.stage[:, late0:late0 + P * nl], T.l[:, P * (R1 + 1):P * N]).then_inc(sem.ldL, 16)
+
+    sent = 0
+    others = [(k, c) for k, c in enumerate(solvers) if c != core]
+
+    def send(pieces, remote_sem):
+        n = 0
+        if len(pieces) == 1:
+            d, src, dst = pieces[0]
+            rid, pid = topo.addr(d, core)
+            m = topo.mask(core, d)
+            g.remote_dma(dst, src, remote_sem, sem.sent, pid, rid, m)
+            return len(_bits(m))
+        common = topo.mask(core, pieces[0][0])
+        for d, _a, _b in pieces:
+            common &= topo.mask(core, d)
+        masks = _split(common, len(pieces))
+        trs = []
+        for (d, src, dst), m in zip(pieces, masks):
+            rid, pid = topo.addr(d, core)
+            trs.append(RemoteDMATransfer(dst_ids=[DstId(rid=rid, pnc=pid)], dma_engine_mask=m,
+                                         remote_sem=remote_sem, src=src, dst=dst))
+            n += len(_bits(m))
+        g.remote_dma_fused(trs, local_sem=sem.sent)
+        return n
+
+    w1 = W + P * ns
+    g.wait_ge(sem.ldE, nE)
+    sent += send([(c, T.stage[:, k * W:k * W + w1], T.land[:, _OFF1[s]:_OFF1[s] + w1]) for k, c in others],
+                 sem["inE%d" % s])
+    if nl:
+        g.wait_ge(sem.ldL, 16)
+        sent += send([(c, T.stage[:, late0:late0 + P * nl], T.land[:, _OFF2[s]:_OFF2[s] + P * nl])
+                      for k, c in others], sem["inL%d" % s])
+
+    if me_k is not None:
+        k = me_k
+
+        def arrives(q, j, late):
+            if j == rank:
+                q.wait_ge(sem.ldL if late else sem.ldE, 16 if late else nE)
+                return
+            src = cores[j]
+            m = len(_bits(topo.mask(src, core)))
+            if src not in solvers:
+                m //= K
+            q.wait_ge(sem[("inL%d" if late else "inE%d") % j], m)
+
+        def b_ap(j):
+            t, base = (T.stage, k * W) if j == rank else (T.land, _OFF1[j])
+            o = base + (0 if k == 0 else P * _ns(j))
+            return t[:, o:o + W]
+
+        def tile_ap(r, j):
+            if j < R1 and r > R1:
+                t, base = (T.stage, late0) if j == rank else (T.land, _OFF2[j])
+                o = base + P * (r - R1 - 1)
+            else:
+                t, base = (T.stage, k * W) if j == rank else (T.land, _OFF1[j])
+                o = base + (W if k == 0 else 0) + P * (r - j - 1)
+            return t[:, o:o + P]
+
+        def y_ap(j):
+            return b_ap(0) if j == 0 else T.ys[:, (j - 1) * W:j * W]
+
+        def mm(r, j):
+            g.tensor.matmul(T["ps%d" % r][:, 0:W], tile_ap(r, j), y_ap(j),
+                            start=(j == 0), stop=(j == r - 1)).then_inc(sem["mm%d" % r], 1)
+
+        for j in range(R1):
+            arrives(g.tensor, j, False)
+            if j:
+                g.tensor.wait_ge(sem["yv%d" % j], 1)
+            for r in range(j + 1, R1 + 1):
+                mm(r, j)
+        for j in range(R1):
+            arrives(g.tensor, j, True)
+            for r in range(R1 + 1, N):
+                mm(r, j)
+        for j in range(R1, N - 1):
+            arrives(g.tensor, j, False)
+            g.tensor.wait_ge(sem["yv%d" % j], 1)
+            for r in range(j + 1, N):
+                mm(r, j)
+
+        for r in range(1, N):
+            arrives(g.vector, r, False)
+            g.vector.wait_ge(sem["mm%d" % r], r)
+            g.vector.tensor_tensor(T.ys[:, (r - 1) * W:r * W], b_ap(r), T["ps%d" % r][:, 0:W],
+                                   AluOpType.subtract).then_inc(sem["yv%d" % r], 1)
+
+        for r in range(1, N):
+            if r == rank:
+                continue
+            g.wait_ge(sem["yv%d" % r], 1)
+            sent += send([(cores[r], T.ys[:, (r - 1) * W:r * W], T.yl[:, k * W:(k + 1) * W])], sem["res%d" % k])
+
+    queues = [g.sync, g.scalar]
+    if rank == 0:
+        g.sync.wait_ge(sem.ldE, nE)
+        g.sync.dma_start(T.y[:], T.b[:]).then_inc(sem.st0, 16)
+        g.sync.wait_ge(sem.st0, 16)
+    else:
+        for k, c in enumerate(solvers):
+            q = queues[k]
+            if c == core:
+                q.wait_ge(sem["yv%d" % rank], 1)
+                src = T.ys[:, (rank - 1) * W:rank * W]
+            else:
+                q.wait_ge(sem["res%d" % k], len(_bits(topo.mask(c, core))))
+                src = T.yl[:, k * W:(k + 1) * W]
+            q.dma_start(T.y[:, k * W:(k + 1) * W], src).then_inc(sem["st%d" % k], 16)
+            q.wait_ge(sem["st%d" % k], 16)
+
+    g.wait_ge(sem.sent, sent)

@@ -4,15 +4,32 @@ from concourse.mybir import AluOpType
 N, P, TK = 9, 128, 512
 K = 2
 W = TK // K
-R1 = 4
+BOUNDS = [2, 5, N - 1]
+NB = len(BOUNDS)
+SIM_CORES = 512
+
+
+def _lo(i):
+    return BOUNDS[i - 1] if i else 0
+
+
+def _f(s):
+    for i in range(NB):
+        if BOUNDS[i] > s:
+            return i
+    return NB - 1
 
 
 def _ns(s):
-    return (R1 - s) if s < R1 else (N - 1 - s)
+    return max(0, BOUNDS[_f(s)] - s)
 
 
 def _nl(s):
-    return (N - 1 - R1) if s < R1 else 0
+    return N - 1 - max(s, BOUNDS[_f(s)])
+
+
+def _piece(r):
+    return [i for i in range(NB) if BOUNDS[i] >= r][0]
 
 
 _OFF1, _OFF2, _c = [], [], 0
@@ -24,7 +41,7 @@ for _s in range(N):
     _c += P * _nl(_s)
 
 SCRATCH = {
-    "stage": ("sbuf", [P, 2 * W + P * (N - 1)], "bfloat16"),
+    "stage": ("sbuf", [P, TK + P * (N - 1)], "bfloat16"),
     "land": ("sbuf", [P, _c], "bfloat16"),
     "ys": ("sbuf", [P, (N - 1) * W], "bfloat16"),
     "yl": ("sbuf", [P, TK], "bfloat16"),
@@ -32,8 +49,8 @@ SCRATCH = {
 for _r in range(1, N):
     SCRATCH["ps%d" % _r] = ("psum", [P, 512], "float32")
 
-SEMAPHORES = (["ldE", "ldL", "sent", "res0", "res1", "st0", "st1"]
-              + ["inE%d" % s for s in range(N)] + ["inL%d" % s for s in range(R1)]
+SEMAPHORES = (["ldE", "ldL", "sent", "hin", "res0", "res1", "st0", "st1"]
+              + ["in%d_%d" % (s, i) for s in range(N) for i in range(_f(s), NB)]
               + ["mm%d" % r for r in range(1, N)] + ["yv%d" % r for r in range(1, N)])
 
 
@@ -48,37 +65,26 @@ def _split(mask, parts):
 
 
 def rank_program(g, core, T, topo):
-    rank = T.rank_of(core)
-    if rank is None:
-        return
     cores = list(T.cores)
     hubs = [c for c in cores
             if all(topo.may_write(c, d) and topo.may_write(d, c) for d in cores if d != c)]
     solvers = hubs[:K]
-    me_k = solvers.index(core) if core in solvers else None
     sem = T.sem
-    s = rank
-    ns, nl = _ns(s), _nl(s)
-    late0 = 2 * W + P * ns
 
-    nE = 32
-    g.sync.dma_start(T.stage[:, 0:W], T.b[:, 0:W]).then_inc(sem.ldE, 16)
-    if ns:
-        g.scalar.dma_start(T.stage[:, W:W + P * ns], T.l[:, P * (s + 1):P * (s + 1 + ns)]).then_inc(sem.ldE, 16)
-        nE += 16
-    g.sync.dma_start(T.stage[:, W + P * ns:late0], T.b[:, W:TK]).then_inc(sem.ldE, 16)
-    if nl:
-        g.scalar.dma_start(T.stage[:, late0:late0 + P * nl], T.l[:, P * (R1 + 1):P * N]).then_inc(sem.ldL, 16)
+    helper = {}
+    for j, c in enumerate(cores):
+        if _nl(j) and topo.rack(topo.host(c)) != topo.rack(topo.host(solvers[0])):
+            cand = [h for h in range(SIM_CORES)
+                    if h != c and topo.host(h) == topo.host(c) and topo.chip(h) == topo.chip(c)
+                    and all(topo.may_write(h, d) for d in solvers)]
+            helper[j] = cand[(1 + 2 * len(helper)) % len(cand)]
 
-    sent = 0
-    others = [(k, c) for k, c in enumerate(solvers) if c != core]
-
-    def send(pieces, remote_sem):
+    def send(pieces, remote_sem, mask=None):
         n = 0
         if len(pieces) == 1:
             d, src, dst = pieces[0]
             rid, pid = topo.addr(d, core)
-            m = topo.mask(core, d)
+            m = mask if mask else topo.mask(core, d)
             g.remote_dma(dst, src, remote_sem, sem.sent, pid, rid, m)
             return len(_bits(m))
         common = topo.mask(core, pieces[0][0])
@@ -94,27 +100,71 @@ def rank_program(g, core, T, topo):
         g.remote_dma_fused(trs, local_sem=sem.sent)
         return n
 
+    def span(j, i):
+        return P * (_lo(i) - BOUNDS[_f(j)]), P * (BOUNDS[i] - BOUNDS[_f(j)])
+
+    def late_call(j, i):
+        a, b = span(j, i)
+        l0 = TK + P * _ns(j)
+        return send([(c, T.stage[:, l0 + a:l0 + b], T.land[:, _OFF2[j] + a:_OFF2[j] + b])
+                     for c in solvers if c != core], sem["in%d_%d" % (j, i)])
+
+    def hand_mask(j):
+        c = cores[j]
+        return topo.mask(c, helper[j]) & ~topo.mask(c, solvers[0])
+
+    rank = T.rank_of(core)
+    if rank is None:
+        for j, h in helper.items():
+            if h == core:
+                g.wait_ge(sem.hin, len(_bits(hand_mask(j))))
+                g.wait_ge(sem.sent, late_call(j, NB - 1))
+        return
+
+    me_k = solvers.index(core) if core in solvers else None
+    s = rank
+    ns, nl, f = _ns(s), _nl(s), _f(s)
+    late0 = TK + P * ns
+
+    nE = 32
+    g.sync.dma_start(T.stage[:, 0:W], T.b[:, 0:W]).then_inc(sem.ldE, 16)
+    if ns:
+        g.scalar.dma_start(T.stage[:, W:W + P * ns], T.l[:, P * (s + 1):P * (s + 1 + ns)]).then_inc(sem.ldE, 16)
+        nE += 16
+    g.sync.dma_start(T.stage[:, W + P * ns:late0], T.b[:, W:TK]).then_inc(sem.ldE, 16)
+    if nl:
+        g.scalar.dma_start(T.stage[:, late0:late0 + P * nl], T.l[:, P * (N - nl):P * N]).then_inc(sem.ldL, 16)
+
+    sent = 0
     w1 = W + P * ns
     g.wait_ge(sem.ldE, nE)
-    sent += send([(c, T.stage[:, k * W:k * W + w1], T.land[:, _OFF1[s]:_OFF1[s] + w1]) for k, c in others],
-                 sem["inE%d" % s])
+    sent += send([(c, T.stage[:, k * W:k * W + w1], T.land[:, _OFF1[s]:_OFF1[s] + w1])
+                  for k, c in enumerate(solvers) if c != core], sem["in%d_%d" % (s, f)])
     if nl:
         g.wait_ge(sem.ldL, 16)
-        sent += send([(c, T.stage[:, late0:late0 + P * nl], T.land[:, _OFF2[s]:_OFF2[s] + P * nl])
-                      for k, c in others], sem["inL%d" % s])
+        if s in helper:
+            a, b = span(s, NB - 1)
+            sent += send([(helper[s], T.stage[:, late0 + a:late0 + b], T.stage[:, late0 + a:late0 + b])],
+                         sem.hin, hand_mask(s))
+        for i in range(f + 1, NB):
+            if not (s in helper and i == NB - 1):
+                sent += late_call(s, i)
 
     if me_k is not None:
         k = me_k
 
-        def arrives(q, j, late):
+        def arrives(q, j, i):
             if j == rank:
-                q.wait_ge(sem.ldL if late else sem.ldE, 16 if late else nE)
+                if i == f:
+                    q.wait_ge(sem.ldE, nE)
+                else:
+                    q.wait_ge(sem.ldL, 16)
                 return
-            src = cores[j]
+            src = helper[j] if (j in helper and i == NB - 1 and i > _f(j)) else cores[j]
             m = len(_bits(topo.mask(src, core)))
             if src not in solvers:
                 m //= K
-            q.wait_ge(sem[("inL%d" if late else "inE%d") % j], m)
+            q.wait_ge(sem["in%d_%d" % (j, i)], m)
 
         def b_ap(j):
             t, base = (T.stage, k * W) if j == rank else (T.land, _OFF1[j])
@@ -122,9 +172,9 @@ def rank_program(g, core, T, topo):
             return t[:, o:o + W]
 
         def tile_ap(r, j):
-            if j < R1 and r > R1:
+            if _piece(r) > _f(j):
                 t, base = (T.stage, late0) if j == rank else (T.land, _OFF2[j])
-                o = base + P * (r - R1 - 1)
+                o = base + P * (r - BOUNDS[_f(j)] - 1)
             else:
                 t, base = (T.stage, k * W) if j == rank else (T.land, _OFF1[j])
                 o = base + (W if k == 0 else 0) + P * (r - j - 1)
@@ -137,24 +187,20 @@ def rank_program(g, core, T, topo):
             g.tensor.matmul(T["ps%d" % r][:, 0:W], tile_ap(r, j), y_ap(j),
                             start=(j == 0), stop=(j == r - 1)).then_inc(sem["mm%d" % r], 1)
 
-        for j in range(R1):
-            arrives(g.tensor, j, False)
-            if j:
-                g.tensor.wait_ge(sem["yv%d" % j], 1)
-            for r in range(j + 1, R1 + 1):
-                mm(r, j)
-        for j in range(R1):
-            arrives(g.tensor, j, True)
-            for r in range(R1 + 1, N):
-                mm(r, j)
-        for j in range(R1, N - 1):
-            arrives(g.tensor, j, False)
-            g.tensor.wait_ge(sem["yv%d" % j], 1)
-            for r in range(j + 1, N):
-                mm(r, j)
+        for i in range(NB):
+            for j in range(_lo(i)):
+                arrives(g.tensor, j, i)
+                for r in range(_lo(i) + 1, BOUNDS[i] + 1):
+                    mm(r, j)
+            for j in range(_lo(i), BOUNDS[i]):
+                arrives(g.tensor, j, i)
+                if j:
+                    g.tensor.wait_ge(sem["yv%d" % j], 1)
+                for r in range(j + 1, BOUNDS[i] + 1):
+                    mm(r, j)
 
         for r in range(1, N):
-            arrives(g.vector, r, False)
+            arrives(g.vector, r, _f(r))
             g.vector.wait_ge(sem["mm%d" % r], r)
             g.vector.tensor_tensor(T.ys[:, (r - 1) * W:r * W], b_ap(r), T["ps%d" % r][:, 0:W],
                                    AluOpType.subtract).then_inc(sem["yv%d" % r], 1)

@@ -4,8 +4,9 @@ from concourse.mybir import AluOpType
 N, P, TK = 9, 128, 512
 K = 2
 W = TK // K
-BOUNDS = [2, 5, N - 1]
+BOUNDS = [2, 4, 6, N - 1]
 NB = len(BOUNDS)
+FIRST_HELPED = 2
 SIM_CORES = 512
 
 
@@ -13,32 +14,14 @@ def _lo(i):
     return BOUNDS[i - 1] if i else 0
 
 
-def _f(s):
-    for i in range(NB):
-        if BOUNDS[i] > s:
-            return i
-    return NB - 1
-
-
-def _ns(s):
-    return max(0, BOUNDS[_f(s)] - s)
-
-
-def _nl(s):
-    return N - 1 - max(s, BOUNDS[_f(s)])
-
-
 def _piece(r):
     return [i for i in range(NB) if BOUNDS[i] >= r][0]
 
 
-_OFF1, _OFF2, _c = [], [], 0
+_OFF, _c = [], 0
 for _s in range(N):
-    _OFF1.append(_c)
-    _c += W + P * _ns(_s)
-for _s in range(N):
-    _OFF2.append(_c)
-    _c += P * _nl(_s)
+    _OFF.append(_c)
+    _c += W + P * (N - 1 - _s)
 
 SCRATCH = {
     "stage": ("sbuf", [P, TK + P * (N - 1)], "bfloat16"),
@@ -50,7 +33,7 @@ for _r in range(1, N):
     SCRATCH["ps%d" % _r] = ("psum", [P, 512], "float32")
 
 SEMAPHORES = (["ldE", "ldL", "sent", "hin", "res0", "res1", "st0", "st1"]
-              + ["in%d_%d" % (s, i) for s in range(N) for i in range(_f(s), NB)]
+              + ["in%d_%d" % (s, i) for s in range(N) for i in range(NB)]
               + ["mm%d" % r for r in range(1, N)] + ["yv%d" % r for r in range(1, N)])
 
 
@@ -70,29 +53,43 @@ def rank_program(g, core, T, topo):
             if all(topo.may_write(c, d) and topo.may_write(d, c) for d in cores if d != c)]
     solvers = hubs[:K]
     sem = T.sem
+    far = [j for j, c in enumerate(cores) if topo.rack(topo.host(c)) != topo.rack(topo.host(solvers[0]))]
+
+    def f_(j):
+        if j in far:
+            return [i for i in range(NB) if BOUNDS[i] > j][0]
+        return NB - 1
+
+    def top(j):
+        return BOUNDS[f_(j)]
+
+    def ns_(j):
+        return top(j) - j
 
     helper = {}
-    for j, c in enumerate(cores):
-        if _nl(j) and topo.rack(topo.host(c)) != topo.rack(topo.host(solvers[0])):
-            cand = [h for h in range(SIM_CORES)
-                    if h != c and topo.host(h) == topo.host(c) and topo.chip(h) == topo.chip(c)
-                    and all(topo.may_write(h, d) for d in solvers)]
-            helper[j] = cand[(1 + 2 * len(helper)) % len(cand)]
+    for n, j in enumerate(far):
+        c = cores[j]
+        cand = [h for h in range(SIM_CORES)
+                if h != c and topo.host(h) == topo.host(c) and topo.chip(h) == topo.chip(c)
+                and all(topo.may_write(h, d) for d in solvers)]
+        reps = cand[1::2]
+        for i in range(max(FIRST_HELPED, f_(j) + 1), NB):
+            helper[(j, i)] = reps[(n + i) % len(reps)]
 
-    def send(pieces, remote_sem, mask=None):
-        n = 0
-        if len(pieces) == 1:
-            d, src, dst = pieces[0]
-            rid, pid = topo.addr(d, core)
-            m = mask if mask else topo.mask(core, d)
-            g.remote_dma(dst, src, remote_sem, sem.sent, pid, rid, m)
-            return len(_bits(m))
+    def send(pieces, remote_sem, within=None):
         common = topo.mask(core, pieces[0][0])
         for d, _a, _b in pieces:
             common &= topo.mask(core, d)
-        masks = _split(common, len(pieces))
+        if within is not None:
+            common &= within
+        if len(pieces) == 1:
+            d, src, dst = pieces[0]
+            rid, pid = topo.addr(d, core)
+            g.remote_dma(dst, src, remote_sem, sem.sent, pid, rid, common)
+            return len(_bits(common))
+        n = 0
         trs = []
-        for (d, src, dst), m in zip(pieces, masks):
+        for (d, src, dst), m in zip(pieces, _split(common, len(pieces))):
             rid, pid = topo.addr(d, core)
             trs.append(RemoteDMATransfer(dst_ids=[DstId(rid=rid, pnc=pid)], dma_engine_mask=m,
                                          remote_sem=remote_sem, src=src, dst=dst))
@@ -100,30 +97,33 @@ def rank_program(g, core, T, topo):
         g.remote_dma_fused(trs, local_sem=sem.sent)
         return n
 
-    def span(j, i):
-        return P * (_lo(i) - BOUNDS[_f(j)]), P * (BOUNDS[i] - BOUNDS[_f(j)])
+    def stage_span(j, i):
+        l0 = TK + P * ns_(j)
+        return l0 + P * (_lo(i) - top(j)), l0 + P * (BOUNDS[i] - top(j))
 
     def late_call(j, i):
-        a, b = span(j, i)
-        l0 = TK + P * _ns(j)
-        return send([(c, T.stage[:, l0 + a:l0 + b], T.land[:, _OFF2[j] + a:_OFF2[j] + b])
-                     for c in solvers if c != core], sem["in%d_%d" % (j, i)])
+        a, b = stage_span(j, i)
+        o = _OFF[j] + W - TK
+        return send([(c, T.stage[:, a:b], T.land[:, o + a:o + b]) for c in solvers if c != core],
+                    sem["in%d_%d" % (j, i)])
 
-    def hand_mask(j):
-        c = cores[j]
-        return topo.mask(c, helper[j]) & ~topo.mask(c, solvers[0])
+    def hand(j):
+        hs = [h for (jj, i), h in helper.items() if jj == j]
+        m = topo.mask(cores[j], hs[0]) & ~topo.mask(cores[j], solvers[0])
+        return m, len(_bits(m)) // len(hs)
 
     rank = T.rank_of(core)
     if rank is None:
-        for j, h in helper.items():
+        for (j, i), h in helper.items():
             if h == core:
-                g.wait_ge(sem.hin, len(_bits(hand_mask(j))))
-                g.wait_ge(sem.sent, late_call(j, NB - 1))
+                g.wait_ge(sem.hin, hand(j)[1])
+                g.wait_ge(sem.sent, late_call(j, i))
         return
 
     me_k = solvers.index(core) if core in solvers else None
     s = rank
-    ns, nl, f = _ns(s), _nl(s), _f(s)
+    f, ns = f_(s), ns_(s)
+    nl = N - 1 - top(s)
     late0 = TK + P * ns
 
     nE = 32
@@ -138,69 +138,73 @@ def rank_program(g, core, T, topo):
     sent = 0
     w1 = W + P * ns
     g.wait_ge(sem.ldE, nE)
-    sent += send([(c, T.stage[:, k * W:k * W + w1], T.land[:, _OFF1[s]:_OFF1[s] + w1])
+    sent += send([(c, T.stage[:, k * W:k * W + w1], T.land[:, _OFF[s]:_OFF[s] + w1])
                   for k, c in enumerate(solvers) if c != core], sem["in%d_%d" % (s, f)])
     if nl:
         g.wait_ge(sem.ldL, 16)
-        if s in helper:
-            a, b = span(s, NB - 1)
-            sent += send([(helper[s], T.stage[:, late0 + a:late0 + b], T.stage[:, late0 + a:late0 + b])],
-                         sem.hin, hand_mask(s))
+        pcs = []
         for i in range(f + 1, NB):
-            if not (s in helper and i == NB - 1):
+            if (s, i) in helper:
+                a, b = stage_span(s, i)
+                pcs.append((helper[(s, i)], T.stage[:, a:b], T.stage[:, a:b]))
+        sent += send(pcs, sem.hin, hand(s)[0])
+        for i in range(f + 1, NB):
+            if (s, i) not in helper:
                 sent += late_call(s, i)
 
     if me_k is not None:
         k = me_k
+        waited = {"t": set(), "v": set()}
 
-        def arrives(q, j, i):
-            if j == rank:
-                if i == f:
-                    q.wait_ge(sem.ldE, nE)
-                else:
-                    q.wait_ge(sem.ldL, 16)
+        def arrives(q, tag, j, i):
+            if (j, i) in waited[tag]:
                 return
-            src = helper[j] if (j in helper and i == NB - 1 and i > _f(j)) else cores[j]
+            waited[tag].add((j, i))
+            if j == rank:
+                q.wait_ge(sem.ldE, nE)
+                return
+            src = helper.get((j, i), cores[j])
             m = len(_bits(topo.mask(src, core)))
             if src not in solvers:
                 m //= K
             q.wait_ge(sem["in%d_%d" % (j, i)], m)
 
         def b_ap(j):
-            t, base = (T.stage, k * W) if j == rank else (T.land, _OFF1[j])
-            o = base + (0 if k == 0 else P * _ns(j))
+            t, base = (T.stage, k * W) if j == rank else (T.land, _OFF[j])
+            o = base + (0 if k == 0 else P * ns_(j))
             return t[:, o:o + W]
 
         def tile_ap(r, j):
-            if _piece(r) > _f(j):
-                t, base = (T.stage, late0) if j == rank else (T.land, _OFF2[j])
-                o = base + P * (r - BOUNDS[_f(j)] - 1)
-            else:
-                t, base = (T.stage, k * W) if j == rank else (T.land, _OFF1[j])
-                o = base + (W if k == 0 else 0) + P * (r - j - 1)
+            if r > top(j):
+                o = _OFF[j] + W + P * (r - j - 1)
+                return T.land[:, o:o + P]
+            t, base = (T.stage, k * W) if j == rank else (T.land, _OFF[j])
+            o = base + (W if k == 0 else 0) + P * (r - j - 1)
             return t[:, o:o + P]
 
         def y_ap(j):
             return b_ap(0) if j == 0 else T.ys[:, (j - 1) * W:j * W]
 
-        def mm(r, j):
-            g.tensor.matmul(T["ps%d" % r][:, 0:W], tile_ap(r, j), y_ap(j),
-                            start=(j == 0), stop=(j == r - 1)).then_inc(sem["mm%d" % r], 1)
-
+        order = []
         for i in range(NB):
-            for j in range(_lo(i)):
-                arrives(g.tensor, j, i)
-                for r in range(_lo(i) + 1, BOUNDS[i] + 1):
-                    mm(r, j)
-            for j in range(_lo(i), BOUNDS[i]):
-                arrives(g.tensor, j, i)
-                if j:
-                    g.tensor.wait_ge(sem["yv%d" % j], 1)
-                for r in range(j + 1, BOUNDS[i] + 1):
-                    mm(r, j)
+            lo, hi = _lo(i), BOUNDS[i]
+            for j in range(lo, hi):
+                order += [(j + 1, a) for a in far if a < lo]
+                order += [(r, j) for r in range(j + 1, (hi if j in far else N - 1) + 1)]
+        count = {}
+        for r, j in order:
+            arrives(g.tensor, "t", j, f_(j))
+            if r > top(j):
+                arrives(g.tensor, "t", j, _piece(r))
+            if j and ("y", j) not in waited["t"]:
+                waited["t"].add(("y", j))
+                g.tensor.wait_ge(sem["yv%d" % j], 1)
+            count[r] = count.get(r, 0) + 1
+            g.tensor.matmul(T["ps%d" % r][:, 0:W], tile_ap(r, j), y_ap(j),
+                            start=(count[r] == 1), stop=(count[r] == r)).then_inc(sem["mm%d" % r], 1)
 
         for r in range(1, N):
-            arrives(g.vector, r, _f(r))
+            arrives(g.vector, "v", r, f_(r))
             g.vector.wait_ge(sem["mm%d" % r], r)
             g.vector.tensor_tensor(T.ys[:, (r - 1) * W:r * W], b_ap(r), T["ps%d" % r][:, 0:W],
                                    AluOpType.subtract).then_inc(sem["yv%d" % r], 1)

@@ -2,12 +2,13 @@ from concourse.bass import DstId, RemoteDMATransfer
 from concourse.mybir import AluOpType
 
 N, P, TK = 9, 128, 512
-K = 2
-W = TK // K
-BOUNDS = [2, 4, 6, N - 1]
+K = 3
+W = 176
+C0 = [0, 168, 336]
+KEEP = [0, 8, 8]
+NA = 3
+BOUNDS = [4, 6, N - 1]
 NB = len(BOUNDS)
-FIRST_HELPED = 2
-SIM_CORES = 512
 
 
 def _lo(i):
@@ -24,17 +25,22 @@ for _s in range(N):
     _c += W + P * (N - 1 - _s)
 
 SCRATCH = {
-    "stage": ("sbuf", [P, TK + P * (N - 1)], "bfloat16"),
+    "stage": ("sbuf", [P, K * W + P * (N - 1)], "bfloat16"),
     "land": ("sbuf", [P, _c], "bfloat16"),
     "ys": ("sbuf", [P, (N - 1) * W], "bfloat16"),
-    "yl": ("sbuf", [P, TK], "bfloat16"),
+    "yl": ("sbuf", [P, K * W], "bfloat16"),
+    "psb": ("sbuf", [P, (N - NA) * W], "bfloat16"),
+    "bp": ("sbuf", [P, (N - NA) * W], "float32"),
 }
 for _r in range(1, N):
     SCRATCH["ps%d" % _r] = ("psum", [P, 512], "float32")
 
-SEMAPHORES = (["ldE", "ldL", "sent", "hin", "res0", "res1", "st0", "st1"]
+SEMAPHORES = (["ldE", "ldL", "ldO", "sent"]
+              + ["res%d" % k for k in range(K)] + ["st%d" % k for k in range(K)]
               + ["in%d_%d" % (s, i) for s in range(N) for i in range(NB)]
-              + ["mm%d" % r for r in range(1, N)] + ["yv%d" % r for r in range(1, N)])
+              + ["pv%d" % i for i in range(NB)] + ["pin%d" % i for i in range(NB)]
+              + ["mm%d" % r for r in range(1, N)] + ["yv%d" % r for r in range(1, N)]
+              + ["bq%d" % r for r in range(1, N)])
 
 
 def _bits(mask):
@@ -48,40 +54,37 @@ def _split(mask, parts):
 
 
 def rank_program(g, core, T, topo):
+    rank = T.rank_of(core)
+    if rank is None:
+        return
     cores = list(T.cores)
+    sem = T.sem
     hubs = [c for c in cores
             if all(topo.may_write(c, d) and topo.may_write(d, c) for d in cores if d != c)]
-    solvers = hubs[:K]
-    sem = T.sem
-    far = [j for j, c in enumerate(cores) if topo.rack(topo.host(c)) != topo.rack(topo.host(solvers[0]))]
+    far = [j for j, c in enumerate(cores) if topo.rack(topo.host(c)) != topo.rack(topo.host(hubs[0]))]
+    sol_a = [cores[j] for j in far]
+    sol_b = [[h for h in hubs if topo.chip(h) == topo.chip(a)][0] for a in sol_a]
 
-    def f_(j):
-        if j in far:
-            return [i for i in range(NB) if BOUNDS[i] > j][0]
-        return NB - 1
+    def site(j):
+        return sol_a if j in far else sol_b
 
     def top(j):
-        return BOUNDS[f_(j)]
+        return BOUNDS[0] if j in far else N - 1
 
     def ns_(j):
         return top(j) - j
 
-    helper = {}
-    for n, j in enumerate(far):
-        c = cores[j]
-        cand = [h for h in range(SIM_CORES)
-                if h != c and topo.host(h) == topo.host(c) and topo.chip(h) == topo.chip(c)
-                and all(topo.may_write(h, d) for d in solvers)]
-        reps = cand[1::2]
-        for i in range(max(FIRST_HELPED, f_(j) + 1), NB):
-            helper[(j, i)] = reps[(n + i) % len(reps)]
+    def dests(j):
+        return [k for k, c in enumerate(site(j)) if c != cores[j]]
 
-    def send(pieces, remote_sem, within=None):
+    def eng(j):
+        d = dests(j)
+        return len(_bits(topo.mask(cores[j], site(j)[d[0]]))) // len(d)
+
+    def send(pieces, remote_sem):
         common = topo.mask(core, pieces[0][0])
         for d, _a, _b in pieces:
             common &= topo.mask(core, d)
-        if within is not None:
-            common &= within
         if len(pieces) == 1:
             d, src, dst = pieces[0]
             rid, pid = topo.addr(d, core)
@@ -97,139 +100,176 @@ def rank_program(g, core, T, topo):
         g.remote_dma_fused(trs, local_sem=sem.sent)
         return n
 
-    def stage_span(j, i):
-        l0 = TK + P * ns_(j)
-        return l0 + P * (_lo(i) - top(j)), l0 + P * (BOUNDS[i] - top(j))
-
-    def late_call(j, i):
-        a, b = stage_span(j, i)
-        o = _OFF[j] + W - TK
-        return send([(c, T.stage[:, a:b], T.land[:, o + a:o + b]) for c in solvers if c != core],
-                    sem["in%d_%d" % (j, i)])
-
-    def hand(j):
-        hs = [h for (jj, i), h in helper.items() if jj == j]
-        m = topo.mask(cores[j], hs[0]) & ~topo.mask(cores[j], solvers[0])
-        return m, len(_bits(m)) // len(hs)
-
-    rank = T.rank_of(core)
-    if rank is None:
-        for (j, i), h in helper.items():
-            if h == core:
-                g.wait_ge(sem.hin, hand(j)[1])
-                g.wait_ge(sem.sent, late_call(j, i))
-        return
-
-    me_k = solvers.index(core) if core in solvers else None
     s = rank
-    f, ns = f_(s), ns_(s)
+    sol = site(s)
+    ds = dests(s)
+    ns = ns_(s)
     nl = N - 1 - top(s)
-    late0 = TK + P * ns
+    w1 = W + P * ns
+    runs = [0, W, 2 * W + P * ns][:len(ds)]
+    late0 = runs[-1] + w1
+    own0 = late0 + P * nl
+    solver = core in sol
 
-    nE = 32
-    g.sync.dma_start(T.stage[:, 0:W], T.b[:, 0:W]).then_inc(sem.ldE, 16)
-    if ns:
-        g.scalar.dma_start(T.stage[:, W:W + P * ns], T.l[:, P * (s + 1):P * (s + 1 + ns)]).then_inc(sem.ldE, 16)
+    nE = 0
+    for n, k in enumerate(ds):
+        o = runs[n] + (0 if n == 0 else P * ns)
+        g.sync.dma_start(T.stage[:, o:o + W], T.b[:, C0[k]:C0[k] + W]).then_inc(sem.ldE, 16)
         nE += 16
-    g.sync.dma_start(T.stage[:, W + P * ns:late0], T.b[:, W:TK]).then_inc(sem.ldE, 16)
+    if ns:
+        for o in [W] + runs[2:]:
+            g.scalar.dma_start(T.stage[:, o:o + P * ns], T.l[:, P * (s + 1):P * (s + 1 + ns)]).then_inc(sem.ldE, 16)
+            nE += 16
     if nl:
         g.scalar.dma_start(T.stage[:, late0:late0 + P * nl], T.l[:, P * (N - nl):P * N]).then_inc(sem.ldL, 16)
+    if solver:
+        kk = sol.index(core)
+        g.sync.dma_start(T.stage[:, own0:own0 + W], T.b[:, C0[kk]:C0[kk] + W]).then_inc(sem.ldO, 16)
 
     sent = 0
-    w1 = W + P * ns
     g.wait_ge(sem.ldE, nE)
-    sent += send([(c, T.stage[:, k * W:k * W + w1], T.land[:, _OFF[s]:_OFF[s] + w1])
-                  for k, c in enumerate(solvers) if c != core], sem["in%d_%d" % (s, f)])
+    sent += send([(sol[k], T.stage[:, runs[n]:runs[n] + w1], T.land[:, _OFF[s]:_OFF[s] + w1])
+                  for n, k in enumerate(ds)], sem["in%d_0" % s])
     if nl:
         g.wait_ge(sem.ldL, 16)
-        pcs = []
-        for i in range(f + 1, NB):
-            if (s, i) in helper:
-                a, b = stage_span(s, i)
-                pcs.append((helper[(s, i)], T.stage[:, a:b], T.stage[:, a:b]))
-        sent += send(pcs, sem.hin, hand(s)[0])
-        for i in range(f + 1, NB):
-            if (s, i) not in helper:
-                sent += late_call(s, i)
+        for i in range(1, NB):
+            a = late0 + P * (_lo(i) - top(s))
+            b = late0 + P * (BOUNDS[i] - top(s))
+            o = _OFF[s] + W + P * (_lo(i) - s)
+            sent += send([(sol[k], T.stage[:, a:b], T.land[:, o:o + b - a]) for k in ds], sem["in%d_%d" % (s, i)])
 
-    if me_k is not None:
-        k = me_k
+    if solver:
+        k = sol.index(core)
+        at_a = s in far
         waited = {"t": set(), "v": set()}
 
+        def once(q, tag, key, sm, val):
+            if key not in waited[tag]:
+                waited[tag].add(key)
+                q.wait_ge(sm, val)
+
         def arrives(q, tag, j, i):
-            if (j, i) in waited[tag]:
-                return
-            waited[tag].add((j, i))
             if j == rank:
-                q.wait_ge(sem.ldE, nE)
-                return
-            src = helper.get((j, i), cores[j])
-            m = len(_bits(topo.mask(src, core)))
-            if src not in solvers:
-                m //= K
-            q.wait_ge(sem["in%d_%d" % (j, i)], m)
+                if i == 0:
+                    once(q, tag, "ldE", sem.ldE, nE)
+                else:
+                    once(q, tag, "ldL", sem.ldL, 16)
+            else:
+                once(q, tag, (j, i), sem["in%d_%d" % (j, i)], eng(j))
+
+        def need_b(q, tag, j):
+            if j == rank:
+                once(q, tag, "ldO", sem.ldO, 16)
+            else:
+                arrives(q, tag, j, 0)
 
         def b_ap(j):
-            t, base = (T.stage, k * W) if j == rank else (T.land, _OFF[j])
-            o = base + (0 if k == 0 else P * ns_(j))
-            return t[:, o:o + W]
+            if j == rank:
+                return T.stage[:, own0:own0 + W]
+            o = _OFF[j] + (0 if dests(j).index(k) == 0 else P * ns_(j))
+            return T.land[:, o:o + W]
 
         def tile_ap(r, j):
+            if j == rank:
+                o = W + P * (r - j - 1) if r <= top(j) else late0 + P * (r - top(j) - 1)
+                return T.stage[:, o:o + P]
             if r > top(j):
                 o = _OFF[j] + W + P * (r - j - 1)
-                return T.land[:, o:o + P]
-            t, base = (T.stage, k * W) if j == rank else (T.land, _OFF[j])
-            o = base + (W if k == 0 else 0) + P * (r - j - 1)
-            return t[:, o:o + P]
+            else:
+                o = _OFF[j] + (W if dests(j).index(k) == 0 else 0) + P * (r - j - 1)
+            return T.land[:, o:o + P]
 
-        def y_ap(j):
-            return b_ap(0) if j == 0 else T.ys[:, (j - 1) * W:j * W]
+        def ys_ap(j):
+            return T.ys[:, (j - 1) * W:j * W]
+
+        def s_ap(r):
+            return T.psb[:, (r - NA) * W:(r - NA + 1) * W]
+
+        def bp_ap(r):
+            return T.bp[:, (r - NA) * W:(r - NA + 1) * W]
 
         order = []
-        for i in range(NB):
-            lo, hi = _lo(i), BOUNDS[i]
-            for j in range(lo, hi):
-                order += [(j + 1, a) for a in far if a < lo]
-                order += [(r, j) for r in range(j + 1, (hi if j in far else N - 1) + 1)]
+        if at_a:
+            for j in range(NA):
+                order += [(r, j) for r in range(j + 1, BOUNDS[0] + 1)]
+            for i in range(1, NB):
+                for r in range(_lo(i) + 1, BOUNDS[i] + 1):
+                    order += [(r, j) for j in range(NA)]
+        else:
+            for j in range(NA, N - 1):
+                order += [(r, j) for r in range(j + 1, N)]
+        total = {}
+        for r, j in order:
+            total[r] = total.get(r, 0) + 1
         count = {}
         for r, j in order:
-            arrives(g.tensor, "t", j, f_(j))
-            if r > top(j):
-                arrives(g.tensor, "t", j, _piece(r))
-            if j and ("y", j) not in waited["t"]:
-                waited["t"].add(("y", j))
-                g.tensor.wait_ge(sem["yv%d" % j], 1)
+            arrives(g.tensor, "t", j, 0 if r <= top(j) else _piece(r))
+            if j == 0:
+                need_b(g.tensor, "t", 0)
+            else:
+                once(g.tensor, "t", ("y", j), sem["yv%d" % j], 1)
             count[r] = count.get(r, 0) + 1
-            g.tensor.matmul(T["ps%d" % r][:, 0:W], tile_ap(r, j), y_ap(j),
-                            start=(count[r] == 1), stop=(count[r] == r)).then_inc(sem["mm%d" % r], 1)
+            g.tensor.matmul(T["ps%d" % r][:, 0:W], tile_ap(r, j), b_ap(0) if j == 0 else ys_ap(j),
+                            start=(count[r] == 1), stop=(count[r] == total[r])).then_inc(sem["mm%d" % r], 1)
 
-        for r in range(1, N):
-            arrives(g.vector, "v", r, f_(r))
-            g.vector.wait_ge(sem["mm%d" % r], r)
-            g.vector.tensor_tensor(T.ys[:, (r - 1) * W:r * W], b_ap(r), T["ps%d" % r][:, 0:W],
-                                   AluOpType.subtract).then_inc(sem["yv%d" % r], 1)
+        if at_a:
+            for r in range(1, N):
+                if r < NA:
+                    need_b(g.vector, "v", r)
+                g.vector.wait_ge(sem["mm%d" % r], total[r])
+                if r < NA:
+                    g.vector.tensor_tensor(ys_ap(r), b_ap(r), T["ps%d" % r][:, 0:W],
+                                           AluOpType.subtract).then_inc(sem["yv%d" % r], 1)
+                else:
+                    g.vector.tensor_copy(s_ap(r), T["ps%d" % r][:, 0:W]).then_inc(sem["pv%d" % _piece(r)], 1)
+            for i in range(NB):
+                rows = list(range(max(NA, _lo(i) + 1), BOUNDS[i] + 1))
+                g.wait_ge(sem["pv%d" % i], len(rows))
+                a, b = (rows[0] - NA) * W, (rows[-1] - NA + 1) * W
+                sent += send([(sol_b[k], T.psb[:, a:b], T.psb[:, a:b])], sem["pin%d" % i])
+                if i == 0:
+                    back = [r for r in range(1, NA) if r != rank]
+                    for r in back:
+                        g.wait_ge(sem["yv%d" % r], 1)
+                    sent += send([(cores[r], ys_ap(r), T.yl[:, k * W:(k + 1) * W]) for r in back], sem["res%d" % k])
+        else:
+            cable = len(_bits(topo.mask(sol_a[k], core)))
+            for r in range(NA, N):
+                need_b(g.vector, "v", r)
+                once(g.vector, "v", ("S", _piece(r)), sem["pin%d" % _piece(r)], cable)
+                if r not in total:
+                    g.vector.tensor_tensor(ys_ap(r), b_ap(r), s_ap(r), AluOpType.subtract).then_inc(sem["yv%d" % r], 1)
+                    continue
+                g.vector.tensor_tensor(bp_ap(r), b_ap(r), s_ap(r), AluOpType.subtract).then_inc(sem["bq%d" % r], 1)
+                g.vector.wait_ge(sem["mm%d" % r], total[r])
+                g.vector.wait_ge(sem["bq%d" % r], 1)
+                g.vector.tensor_tensor(ys_ap(r), bp_ap(r), T["ps%d" % r][:, 0:W],
+                                       AluOpType.subtract).then_inc(sem["yv%d" % r], 1)
+            for r in range(NA, N):
+                if r == rank:
+                    continue
+                g.wait_ge(sem["yv%d" % r], 1)
+                sent += send([(cores[r], ys_ap(r), T.yl[:, k * W:(k + 1) * W])], sem["res%d" % k])
 
-        for r in range(1, N):
-            if r == rank:
-                continue
-            g.wait_ge(sem["yv%d" % r], 1)
-            sent += send([(cores[r], T.ys[:, (r - 1) * W:r * W], T.yl[:, k * W:(k + 1) * W])], sem["res%d" % k])
-
-    queues = [g.sync, g.scalar]
     if rank == 0:
         g.sync.wait_ge(sem.ldE, nE)
         g.sync.dma_start(T.y[:], T.b[:]).then_inc(sem.st0, 16)
         g.sync.wait_ge(sem.st0, 16)
     else:
-        for k, c in enumerate(solvers):
+        queues = [g.sync, g.scalar, g.sync]
+        for k, c in enumerate(sol):
             q = queues[k]
             if c == core:
                 q.wait_ge(sem["yv%d" % rank], 1)
-                src = T.ys[:, (rank - 1) * W:rank * W]
+                src = T.ys[:, (rank - 1) * W + KEEP[k]:rank * W]
             else:
-                q.wait_ge(sem["res%d" % k], len(_bits(topo.mask(c, core))))
-                src = T.yl[:, k * W:(k + 1) * W]
-            q.dma_start(T.y[:, k * W:(k + 1) * W], src).then_inc(sem["st%d" % k], 16)
-            q.wait_ge(sem["st%d" % k], 16)
+                m = len(_bits(topo.mask(c, core)))
+                if rank in far:
+                    m //= len([r for r in range(1, NA) if cores[r] != c])
+                q.wait_ge(sem["res%d" % k], m)
+                src = T.yl[:, k * W + KEEP[k]:(k + 1) * W]
+            q.dma_start(T.y[:, C0[k] + KEEP[k]:C0[k] + W], src).then_inc(sem["st%d" % k], 16)
+        for k in range(K):
+            queues[k].wait_ge(sem["st%d" % k], 16)
 
     g.wait_ge(sem.sent, sent)

@@ -7,7 +7,7 @@ W = 176
 C0 = [0, 168, 336]
 KEEP = [0, 8, 8]
 NA = 3
-BOUNDS = [4, 6, N - 1]
+BOUNDS = [3, 5, 7, N - 1]
 NB = len(BOUNDS)
 
 

@@ -2,13 +2,17 @@ from concourse.bass import DstId, RemoteDMATransfer
 from concourse.mybir import AluOpType
 
 N, P, TK = 9, 128, 512
+WORLD = 512
 K = 3
 W = 176
 C0 = [0, 168, 336]
 KEEP = [0, 8, 8]
 NA = 3
-BOUNDS = [3, 5, 7, N - 1]
+BOUNDS = [3, 4]
 NB = len(BOUNDS)
+HROWS = [[5, 6], [7, 8]]
+NH = len(HROWS)
+HT = len(HROWS[0])
 
 
 def _lo(i):
@@ -27,19 +31,22 @@ for _s in range(N):
 SCRATCH = {
     "stage": ("sbuf", [P, K * W + P * (N - 1)], "bfloat16"),
     "land": ("sbuf", [P, _c], "bfloat16"),
-    "ys": ("sbuf", [P, (N - 1) * W], "bfloat16"),
+    "ys": ("sbuf", [P, N * W], "bfloat16"),
     "yl": ("sbuf", [P, K * W], "bfloat16"),
     "psb": ("sbuf", [P, (N - NA) * W], "bfloat16"),
     "bp": ("sbuf", [P, (N - NA) * W], "float32"),
+    "ht": ("sbuf", [P, NA * HT * P], "bfloat16"),
+    "hy": ("sbuf", [P, NA * W], "bfloat16"),
 }
 for _r in range(1, N):
     SCRATCH["ps%d" % _r] = ("psum", [P, 512], "float32")
 
-SEMAPHORES = (["ldE", "ldL", "ldO", "sent"]
+SEMAPHORES = (["ldE", "ldL", "ldO", "sent", "yf"]
               + ["res%d" % k for k in range(K)] + ["st%d" % k for k in range(K)]
               + ["in%d_%d" % (s, i) for s in range(N) for i in range(NB)]
-              + ["pv%d" % i for i in range(NB)] + ["pin%d" % i for i in range(NB)]
-              + ["mm%d" % r for r in range(1, N)] + ["yv%d" % r for r in range(1, N)]
+              + ["hin%d" % s for s in range(NA)]
+              + ["pv%d" % r for r in range(NA, N)] + ["pin%d" % r for r in range(NA, N)]
+              + ["mm%d" % r for r in range(1, N)] + ["yv%d" % r for r in range(N)]
               + ["bq%d" % r for r in range(1, N)])
 
 
@@ -55,8 +62,6 @@ def _split(mask, parts):
 
 def rank_program(g, core, T, topo):
     rank = T.rank_of(core)
-    if rank is None:
-        return
     cores = list(T.cores)
     sem = T.sem
     hubs = [c for c in cores
@@ -64,6 +69,72 @@ def rank_program(g, core, T, topo):
     far = [j for j, c in enumerate(cores) if topo.rack(topo.host(c)) != topo.rack(topo.host(hubs[0]))]
     sol_a = [cores[j] for j in far]
     sol_b = [[h for h in hubs if topo.chip(h) == topo.chip(a)][0] for a in sol_a]
+
+    def helpers_of(c):
+        mate = [x for x in range(WORLD) if topo.mates(c, x)][0]
+        other = [x for x in range(WORLD) if topo.host(x) == topo.host(c) and topo.chip(x) == topo.chip(c)
+                 and topo.die(x) != topo.die(c)]
+        return [[x for x in other if topo.may_write(x, mate)][0], [x for x in other if not topo.may_write(x, mate)][0]]
+
+    helpers = [helpers_of(c) for c in sol_a]
+    role = [(k, h) for k in range(K) for h in range(NH) if helpers[k][h] == core]
+    if rank is None and not role:
+        return
+
+    def chip_only(k):
+        return topo.mask(sol_a[k], helpers[k][0]) & ~topo.mask(sol_a[k], sol_b[k])
+
+    def send(pieces, remote_sem, within=None):
+        common = topo.mask(core, pieces[0][0])
+        for d, _a, _b in pieces:
+            common &= topo.mask(core, d)
+        if within is not None:
+            common &= within
+        if len(pieces) == 1:
+            d, src, dst = pieces[0]
+            rid, pid = topo.addr(d, core)
+            g.remote_dma(dst, src, remote_sem, sem.sent, pid, rid, common)
+            return len(_bits(common))
+        n = 0
+        trs = []
+        for (d, src, dst), m in zip(pieces, _split(common, len(pieces))):
+            rid, pid = topo.addr(d, core)
+            trs.append(RemoteDMATransfer(dst_ids=[DstId(rid=rid, pnc=pid)], dma_engine_mask=m,
+                                         remote_sem=remote_sem, src=src, dst=dst))
+            n += len(_bits(m))
+        g.remote_dma_fused(trs, local_sem=sem.sent)
+        return n
+
+    def s_ap(r):
+        return T.psb[:, (r - NA) * W:(r - NA + 1) * W]
+
+    if role:
+        k, h = role[0]
+        rows = HROWS[h]
+        own = far[k]
+        n_loc = len(_bits(chip_only(k))) // NH
+        peers = [helpers[x][h] for x in range(K) if x != k]
+        n_peer = len(_bits(topo.mask(peers[0], core))) // len(peers)
+        slot = T.ht[:, own * HT * P:(own + 1) * HT * P]
+        sent = 0
+        g.wait_ge(sem["hin%d" % own], n_loc)
+        sent += send([(p, slot, slot) for p in peers], sem["hin%d" % own])
+        for j in far:
+            g.tensor.wait_ge(sem["hin%d" % j], n_loc if j == own else n_peer)
+        g.tensor.wait_ge(sem.yf, n_loc)
+        for i, r in enumerate(rows):
+            for j in far:
+                o = (j * HT + i) * P
+                g.tensor.matmul(T["ps%d" % r][:, 0:W], T.ht[:, o:o + P], T.hy[:, j * W:(j + 1) * W],
+                                start=(j == far[0]), stop=(j == far[-1])).then_inc(sem["mm%d" % r], 1)
+        for r in rows:
+            g.vector.wait_ge(sem["mm%d" % r], len(far))
+            g.vector.tensor_copy(s_ap(r), T["ps%d" % r][:, 0:W]).then_inc(sem["pv%d" % r], 1)
+        for r in rows:
+            g.wait_ge(sem["pv%d" % r], 1)
+            sent += send([(sol_b[k], s_ap(r), s_ap(r))], sem["pin%d" % r])
+        g.wait_ge(sem.sent, sent)
+        return
 
     def site(j):
         return sol_a if j in far else sol_b
@@ -80,25 +151,6 @@ def rank_program(g, core, T, topo):
     def eng(j):
         d = dests(j)
         return len(_bits(topo.mask(cores[j], site(j)[d[0]]))) // len(d)
-
-    def send(pieces, remote_sem):
-        common = topo.mask(core, pieces[0][0])
-        for d, _a, _b in pieces:
-            common &= topo.mask(core, d)
-        if len(pieces) == 1:
-            d, src, dst = pieces[0]
-            rid, pid = topo.addr(d, core)
-            g.remote_dma(dst, src, remote_sem, sem.sent, pid, rid, common)
-            return len(_bits(common))
-        n = 0
-        trs = []
-        for (d, src, dst), m in zip(pieces, _split(common, len(pieces))):
-            rid, pid = topo.addr(d, core)
-            trs.append(RemoteDMATransfer(dst_ids=[DstId(rid=rid, pnc=pid)], dma_engine_mask=m,
-                                         remote_sem=remote_sem, src=src, dst=dst))
-            n += len(_bits(m))
-        g.remote_dma_fused(trs, local_sem=sem.sent)
-        return n
 
     s = rank
     sol = site(s)
@@ -132,6 +184,12 @@ def rank_program(g, core, T, topo):
                   for n, k in enumerate(ds)], sem["in%d_0" % s])
     if nl:
         g.wait_ge(sem.ldL, 16)
+        ka = sol.index(core)
+        hp = []
+        for h in range(NH):
+            a = late0 + P * (HROWS[h][0] - top(s) - 1)
+            hp.append((helpers[ka][h], T.stage[:, a:a + HT * P], T.ht[:, s * HT * P:(s + 1) * HT * P]))
+        sent += send(hp, sem["hin%d" % s], within=chip_only(ka))
         for i in range(1, NB):
             a = late0 + P * (_lo(i) - top(s))
             b = late0 + P * (BOUNDS[i] - top(s))
@@ -180,10 +238,7 @@ def rank_program(g, core, T, topo):
             return T.land[:, o:o + P]
 
         def ys_ap(j):
-            return T.ys[:, (j - 1) * W:j * W]
-
-        def s_ap(r):
-            return T.psb[:, (r - NA) * W:(r - NA + 1) * W]
+            return T.ys[:, j * W:(j + 1) * W]
 
         def bp_ap(r):
             return T.bp[:, (r - NA) * W:(r - NA + 1) * W]
@@ -213,7 +268,9 @@ def rank_program(g, core, T, topo):
                             start=(count[r] == 1), stop=(count[r] == total[r])).then_inc(sem["mm%d" % r], 1)
 
         if at_a:
-            for r in range(1, N):
+            need_b(g.vector, "v", 0)
+            g.vector.tensor_copy(ys_ap(0), b_ap(0)).then_inc(sem.yv0, 1)
+            for r in range(1, BOUNDS[-1] + 1):
                 if r < NA:
                     need_b(g.vector, "v", r)
                 g.vector.wait_ge(sem["mm%d" % r], total[r])
@@ -221,22 +278,24 @@ def rank_program(g, core, T, topo):
                     g.vector.tensor_tensor(ys_ap(r), b_ap(r), T["ps%d" % r][:, 0:W],
                                            AluOpType.subtract).then_inc(sem["yv%d" % r], 1)
                 else:
-                    g.vector.tensor_copy(s_ap(r), T["ps%d" % r][:, 0:W]).then_inc(sem["pv%d" % _piece(r)], 1)
-            for i in range(NB):
-                rows = list(range(max(NA, _lo(i) + 1), BOUNDS[i] + 1))
-                g.wait_ge(sem["pv%d" % i], len(rows))
-                a, b = (rows[0] - NA) * W, (rows[-1] - NA + 1) * W
-                sent += send([(sol_b[k], T.psb[:, a:b], T.psb[:, a:b])], sem["pin%d" % i])
-                if i == 0:
-                    back = [r for r in range(1, NA) if r != rank]
-                    for r in back:
-                        g.wait_ge(sem["yv%d" % r], 1)
-                    sent += send([(cores[r], ys_ap(r), T.yl[:, k * W:(k + 1) * W]) for r in back], sem["res%d" % k])
+                    g.vector.tensor_copy(s_ap(r), T["ps%d" % r][:, 0:W]).then_inc(sem["pv%d" % r], 1)
+            for j in range(NA):
+                g.wait_ge(sem["yv%d" % j], 1)
+            sent += send([(helpers[k][h], T.ys[:, 0:NA * W], T.hy[:, 0:NA * W]) for h in range(NH)],
+                         sem.yf, within=chip_only(k))
+            for r in range(NA, BOUNDS[-1] + 1):
+                g.wait_ge(sem["pv%d" % r], 1)
+                sent += send([(sol_b[k], s_ap(r), s_ap(r))], sem["pin%d" % r])
+            back = [r for r in range(1, NA) if r != rank]
+            sent += send([(cores[r], ys_ap(r), T.yl[:, k * W:(k + 1) * W]) for r in back], sem["res%d" % k])
         else:
-            cable = len(_bits(topo.mask(sol_a[k], core)))
+            maker = {r: sol_a[k] for r in range(NA, BOUNDS[-1] + 1)}
+            for h in range(NH):
+                for r in HROWS[h]:
+                    maker[r] = helpers[k][h]
             for r in range(NA, N):
                 need_b(g.vector, "v", r)
-                once(g.vector, "v", ("S", _piece(r)), sem["pin%d" % _piece(r)], cable)
+                g.vector.wait_ge(sem["pin%d" % r], len(_bits(topo.mask(maker[r], core))))
                 if r not in total:
                     g.vector.tensor_tensor(ys_ap(r), b_ap(r), s_ap(r), AluOpType.subtract).then_inc(sem["yv%d" % r], 1)
                     continue
@@ -261,7 +320,7 @@ def rank_program(g, core, T, topo):
             q = queues[k]
             if c == core:
                 q.wait_ge(sem["yv%d" % rank], 1)
-                src = T.ys[:, (rank - 1) * W + KEEP[k]:rank * W]
+                src = T.ys[:, rank * W + KEEP[k]:(rank + 1) * W]
             else:
                 m = len(_bits(topo.mask(c, core)))
                 if rank in far:

@@ -10,6 +10,7 @@ KEEP = [0, 8, 8]
 NA = 3
 BOUNDS = [3, 4]
 NB = len(BOUNDS)
+BOUND_B = 6
 HROWS = [[5, 6], [7, 8]]
 NH = len(HROWS)
 HT = len(HROWS[0])
@@ -34,20 +35,20 @@ SCRATCH = {
     "ys": ("sbuf", [P, N * W], "bfloat16"),
     "yl": ("sbuf", [P, K * W], "bfloat16"),
     "psb": ("sbuf", [P, (N - NA) * W], "bfloat16"),
-    "bp": ("sbuf", [P, (N - NA) * W], "float32"),
     "ht": ("sbuf", [P, NA * HT * P], "bfloat16"),
     "hy": ("sbuf", [P, NA * W], "bfloat16"),
+    "neg1": ("sbuf", [P, P], "bfloat16"),
+    "negI": ("sbuf", [P, P], "bfloat16"),
 }
 for _r in range(1, N):
     SCRATCH["ps%d" % _r] = ("psum", [P, 512], "float32")
 
-SEMAPHORES = (["ldE", "ldL", "ldO", "sent", "yf"]
+SEMAPHORES = (["ldE", "ldL", "ldO", "sent", "yfa", "yfb", "c1", "c2"]
               + ["res%d" % k for k in range(K)] + ["st%d" % k for k in range(K)]
               + ["in%d_%d" % (s, i) for s in range(N) for i in range(NB)]
               + ["hin%d" % s for s in range(NA)]
               + ["pv%d" % r for r in range(NA, N)] + ["pin%d" % r for r in range(NA, N)]
-              + ["mm%d" % r for r in range(1, N)] + ["yv%d" % r for r in range(N)]
-              + ["bq%d" % r for r in range(1, N)])
+              + ["mm%d" % r for r in range(1, N)] + ["yv%d" % r for r in range(N)])
 
 
 def _bits(mask):
@@ -108,6 +109,9 @@ def rank_program(g, core, T, topo):
     def s_ap(r):
         return T.psb[:, (r - NA) * W:(r - NA + 1) * W]
 
+    def minus_sum(r):
+        g.vector.tensor_scalar(s_ap(r), T["ps%d" % r][:, 0:W], -1.0, None, AluOpType.mult).then_inc(sem["pv%d" % r], 1)
+
     if role:
         k, h = role[0]
         rows = HROWS[h]
@@ -119,17 +123,18 @@ def rank_program(g, core, T, topo):
         sent = 0
         g.wait_ge(sem["hin%d" % own], n_loc)
         sent += send([(p, slot, slot) for p in peers], sem["hin%d" % own])
-        for j in far:
-            g.tensor.wait_ge(sem["hin%d" % j], n_loc if j == own else n_peer)
-        g.tensor.wait_ge(sem.yf, n_loc)
-        for i, r in enumerate(rows):
-            for j in far:
-                o = (j * HT + i) * P
-                g.tensor.matmul(T["ps%d" % r][:, 0:W], T.ht[:, o:o + P], T.hy[:, j * W:(j + 1) * W],
-                                start=(j == far[0]), stop=(j == far[-1])).then_inc(sem["mm%d" % r], 1)
+        for part, ysem in ((far[:-1], sem.yfa), (far[-1:], sem.yfb)):
+            for j in part:
+                g.tensor.wait_ge(sem["hin%d" % j], n_loc if j == own else n_peer)
+            g.tensor.wait_ge(ysem, n_loc)
+            for i, r in enumerate(rows):
+                for j in part:
+                    o = (j * HT + i) * P
+                    g.tensor.matmul(T["ps%d" % r][:, 0:W], T.ht[:, o:o + P], T.hy[:, j * W:(j + 1) * W],
+                                    start=(j == far[0]), stop=(j == far[-1])).then_inc(sem["mm%d" % r], 1)
         for r in rows:
             g.vector.wait_ge(sem["mm%d" % r], len(far))
-            g.vector.tensor_copy(s_ap(r), T["ps%d" % r][:, 0:W]).then_inc(sem["pv%d" % r], 1)
+            minus_sum(r)
         for r in rows:
             g.wait_ge(sem["pv%d" % r], 1)
             sent += send([(sol_b[k], s_ap(r), s_ap(r))], sem["pin%d" % r])
@@ -140,7 +145,12 @@ def rank_program(g, core, T, topo):
         return sol_a if j in far else sol_b
 
     def top(j):
-        return BOUNDS[0] if j in far else N - 1
+        return BOUNDS[0] if j in far else max(BOUND_B, j)
+
+    def piece_of(r, j):
+        if r <= top(j):
+            return 0
+        return _piece(r) if j in far else 1
 
     def ns_(j):
         return top(j) - j
@@ -177,6 +187,10 @@ def rank_program(g, core, T, topo):
     if solver:
         kk = sol.index(core)
         g.sync.dma_start(T.stage[:, own0:own0 + W], T.b[:, C0[kk]:C0[kk] + W]).then_inc(sem.ldO, 16)
+    if solver and s not in far:
+        g.vector.memset(T.neg1[:], -1.0).then_inc(sem.c1, 1)
+        g.wait_ge(sem.c1, 1)
+        g.affine_select(T.negI[:], T.neg1[:], [[-1, P]], AluOpType.is_equal, 0.0, 0, 1).then_inc(sem.c2, 1)
 
     sent = 0
     g.wait_ge(sem.ldE, nE)
@@ -184,16 +198,20 @@ def rank_program(g, core, T, topo):
                   for n, k in enumerate(ds)], sem["in%d_0" % s])
     if nl:
         g.wait_ge(sem.ldL, 16)
-        ka = sol.index(core)
-        hp = []
-        for h in range(NH):
-            a = late0 + P * (HROWS[h][0] - top(s) - 1)
-            hp.append((helpers[ka][h], T.stage[:, a:a + HT * P], T.ht[:, s * HT * P:(s + 1) * HT * P]))
-        sent += send(hp, sem["hin%d" % s], within=chip_only(ka))
-        for i in range(1, NB):
-            a = late0 + P * (_lo(i) - top(s))
-            b = late0 + P * (BOUNDS[i] - top(s))
-            o = _OFF[s] + W + P * (_lo(i) - s)
+        if s in far:
+            ka = sol.index(core)
+            hp = []
+            for h in range(NH):
+                a = late0 + P * (HROWS[h][0] - top(s) - 1)
+                hp.append((helpers[ka][h], T.stage[:, a:a + HT * P], T.ht[:, s * HT * P:(s + 1) * HT * P]))
+            sent += send(hp, sem["hin%d" % s], within=chip_only(ka))
+            later = [(i, _lo(i), BOUNDS[i]) for i in range(1, NB)]
+        else:
+            later = [(1, top(s), N - 1)]
+        for i, lo, hi in later:
+            a = late0 + P * (lo - top(s))
+            b = late0 + P * (hi - top(s))
+            o = _OFF[s] + W + P * (lo - s)
             sent += send([(sol[k], T.stage[:, a:b], T.land[:, o:o + b - a]) for k in ds], sem["in%d_%d" % (s, i)])
 
     if solver:
@@ -240,9 +258,6 @@ def rank_program(g, core, T, topo):
         def ys_ap(j):
             return T.ys[:, j * W:(j + 1) * W]
 
-        def bp_ap(r):
-            return T.bp[:, (r - NA) * W:(r - NA + 1) * W]
-
         order = []
         if at_a:
             for j in range(NA):
@@ -251,20 +266,32 @@ def rank_program(g, core, T, topo):
                 for r in range(_lo(i) + 1, BOUNDS[i] + 1):
                     order += [(r, j) for j in range(NA)]
         else:
-            for j in range(NA, N - 1):
+            order += [(r, None) for r in range(NA, N)]
+            first = list(range(NA, BOUNDS[-1] + 1))
+            for j in first:
+                order += [(r, j) for r in range(j + 1, BOUND_B + 1)]
+            for j in first:
+                order += [(r, j) for r in range(BOUND_B + 1, N)]
+            for j in range(first[-1] + 1, N - 1):
                 order += [(r, j) for r in range(j + 1, N)]
         total = {}
         for r, j in order:
             total[r] = total.get(r, 0) + 1
         count = {}
         for r, j in order:
-            arrives(g.tensor, "t", j, 0 if r <= top(j) else _piece(r))
-            if j == 0:
-                need_b(g.tensor, "t", 0)
-            else:
-                once(g.tensor, "t", ("y", j), sem["yv%d" % j], 1)
             count[r] = count.get(r, 0) + 1
-            g.tensor.matmul(T["ps%d" % r][:, 0:W], tile_ap(r, j), b_ap(0) if j == 0 else ys_ap(j),
+            if j is None:
+                once(g.tensor, "t", "c2", sem.c2, 1)
+                need_b(g.tensor, "t", r)
+                lhs, rhs = T.negI[:], b_ap(r)
+            else:
+                arrives(g.tensor, "t", j, piece_of(r, j))
+                if j == 0:
+                    need_b(g.tensor, "t", 0)
+                else:
+                    once(g.tensor, "t", ("y", j), sem["yv%d" % j], 1)
+                lhs, rhs = tile_ap(r, j), (b_ap(0) if j == 0 else ys_ap(j))
+            g.tensor.matmul(T["ps%d" % r][:, 0:W], lhs, rhs,
                             start=(count[r] == 1), stop=(count[r] == total[r])).then_inc(sem["mm%d" % r], 1)
 
         if at_a:
@@ -278,11 +305,12 @@ def rank_program(g, core, T, topo):
                     g.vector.tensor_tensor(ys_ap(r), b_ap(r), T["ps%d" % r][:, 0:W],
                                            AluOpType.subtract).then_inc(sem["yv%d" % r], 1)
                 else:
-                    g.vector.tensor_copy(s_ap(r), T["ps%d" % r][:, 0:W]).then_inc(sem["pv%d" % r], 1)
-            for j in range(NA):
-                g.wait_ge(sem["yv%d" % j], 1)
-            sent += send([(helpers[k][h], T.ys[:, 0:NA * W], T.hy[:, 0:NA * W]) for h in range(NH)],
-                         sem.yf, within=chip_only(k))
+                    minus_sum(r)
+            for lo, hi, ysem in ((0, NA - 1, sem.yfa), (NA - 1, NA, sem.yfb)):
+                for j in range(lo, hi):
+                    g.wait_ge(sem["yv%d" % j], 1)
+                sent += send([(helpers[k][h], T.ys[:, lo * W:hi * W], T.hy[:, lo * W:hi * W]) for h in range(NH)],
+                             ysem, within=chip_only(k))
             for r in range(NA, BOUNDS[-1] + 1):
                 g.wait_ge(sem["pv%d" % r], 1)
                 sent += send([(sol_b[k], s_ap(r), s_ap(r))], sem["pin%d" % r])
@@ -294,15 +322,9 @@ def rank_program(g, core, T, topo):
                 for r in HROWS[h]:
                     maker[r] = helpers[k][h]
             for r in range(NA, N):
-                need_b(g.vector, "v", r)
                 g.vector.wait_ge(sem["pin%d" % r], len(_bits(topo.mask(maker[r], core))))
-                if r not in total:
-                    g.vector.tensor_tensor(ys_ap(r), b_ap(r), s_ap(r), AluOpType.subtract).then_inc(sem["yv%d" % r], 1)
-                    continue
-                g.vector.tensor_tensor(bp_ap(r), b_ap(r), s_ap(r), AluOpType.subtract).then_inc(sem["bq%d" % r], 1)
                 g.vector.wait_ge(sem["mm%d" % r], total[r])
-                g.vector.wait_ge(sem["bq%d" % r], 1)
-                g.vector.tensor_tensor(ys_ap(r), bp_ap(r), T["ps%d" % r][:, 0:W],
+                g.vector.tensor_tensor(ys_ap(r), s_ap(r), T["ps%d" % r][:, 0:W],
                                        AluOpType.subtract).then_inc(sem["yv%d" % r], 1)
             for r in range(NA, N):
                 if r == rank:

@@ -8,20 +8,19 @@ W = 176
 C0 = [0, 168, 336]
 KEEP = [0, 8, 8]
 NA = 3
-BOUNDS = [3, 4]
-NB = len(BOUNDS)
+APIECES = [(1, 2), (3, 4)]
+NB = len(APIECES)
+SROWS = [3, 4]
+EARLY = [3, 4]
 BOUND_B = 6
-HROWS = [[5, 6], [7, 8]]
+HROWS = [[5, 8], [6], [7]]
 NH = len(HROWS)
-HT = len(HROWS[0])
-
-
-def _lo(i):
-    return BOUNDS[i - 1] if i else 0
+HT = max(len(_x) for _x in HROWS)
+TSEM = ["hin%d", "hjn%d"]
 
 
 def _piece(r):
-    return [i for i in range(NB) if BOUNDS[i] >= r][0]
+    return [i for i in range(NB) if APIECES[i][0] <= r <= APIECES[i][1]][0]
 
 
 _OFF, _c = [], 0
@@ -46,7 +45,7 @@ for _r in range(1, N):
 SEMAPHORES = (["ldE", "ldL", "ldO", "sent", "yfa", "yfb", "c1", "c2"]
               + ["res%d" % k for k in range(K)] + ["st%d" % k for k in range(K)]
               + ["in%d_%d" % (s, i) for s in range(N) for i in range(NB)]
-              + ["hin%d" % s for s in range(NA)]
+              + [t % s for s in range(NA) for t in TSEM]
               + ["pv%d" % r for r in range(NA, N)] + ["pin%d" % r for r in range(NA, N)]
               + ["mm%d" % r for r in range(1, N)] + ["yv%d" % r for r in range(N)])
 
@@ -55,9 +54,15 @@ def _bits(mask):
     return [1 << i for i in range(mask.bit_length()) if (mask >> i) & 1]
 
 
-def _split(mask, parts):
-    e = _bits(mask)
-    n = len(e) // parts
+def _share(n_eng, parts):
+    n = 1
+    while 2 * n * parts <= n_eng:
+        n *= 2
+    return n
+
+
+def _deal(e, parts):
+    n = _share(len(e), parts)
     return [sum(e[i * n:(i + 1) * n]) for i in range(parts)]
 
 
@@ -73,9 +78,11 @@ def rank_program(g, core, T, topo):
 
     def helpers_of(c):
         mate = [x for x in range(WORLD) if topo.mates(c, x)][0]
-        other = [x for x in range(WORLD) if topo.host(x) == topo.host(c) and topo.chip(x) == topo.chip(c)
-                 and topo.die(x) != topo.die(c)]
-        return [[x for x in other if topo.may_write(x, mate)][0], [x for x in other if not topo.may_write(x, mate)][0]]
+        chip = [x for x in range(WORLD) if topo.host(x) == topo.host(c) and topo.chip(x) == topo.chip(c)]
+        other = [x for x in chip if topo.die(x) != topo.die(c)]
+        same = [x for x in chip if topo.die(x) == topo.die(c)]
+        return [[x for x in other if topo.may_write(x, mate)][0], [x for x in other if not topo.may_write(x, mate)][0],
+                [x for x in same if topo.may_write(x, mate) != topo.may_write(c, mate)][0]]
 
     helpers = [helpers_of(c) for c in sol_a]
     role = [(k, h) for k in range(K) for h in range(NH) if helpers[k][h] == core]
@@ -85,12 +92,13 @@ def rank_program(g, core, T, topo):
     def chip_only(k):
         return topo.mask(sol_a[k], helpers[k][0]) & ~topo.mask(sol_a[k], sol_b[k])
 
-    def send(pieces, remote_sem, within=None):
+    def send(pieces, remote_sem, first=0, only=None):
         common = topo.mask(core, pieces[0][0])
         for d, _a, _b in pieces:
             common &= topo.mask(core, d)
-        if within is not None:
-            common &= within
+        if only is not None:
+            common &= only
+        e = [x for x in _bits(common) if x & first] + [x for x in _bits(common) if not x & first]
         if len(pieces) == 1:
             d, src, dst = pieces[0]
             rid, pid = topo.addr(d, core)
@@ -98,7 +106,7 @@ def rank_program(g, core, T, topo):
             return len(_bits(common))
         n = 0
         trs = []
-        for (d, src, dst), m in zip(pieces, _split(common, len(pieces))):
+        for (d, src, dst), m in zip(pieces, _deal(e, len(pieces))):
             rid, pid = topo.addr(d, core)
             trs.append(RemoteDMATransfer(dst_ids=[DstId(rid=rid, pnc=pid)], dma_engine_mask=m,
                                          remote_sem=remote_sem, src=src, dst=dst))
@@ -109,6 +117,9 @@ def rank_program(g, core, T, topo):
     def s_ap(r):
         return T.psb[:, (r - NA) * W:(r - NA + 1) * W]
 
+    def ht_ap(j, i):
+        return T.ht[:, (j * HT + i) * P:(j * HT + i + 1) * P]
+
     def minus_sum(r):
         g.vector.tensor_scalar(s_ap(r), T["ps%d" % r][:, 0:W], -1.0, None, AluOpType.mult).then_inc(sem["pv%d" % r], 1)
 
@@ -116,21 +127,22 @@ def rank_program(g, core, T, topo):
         k, h = role[0]
         rows = HROWS[h]
         own = far[k]
-        n_loc = len(_bits(chip_only(k))) // NH
+        n_fwd = _share(len(_bits(topo.mask(sol_a[k], core))), NH)
+        n_loc = [n_fwd, len(_bits(chip_only(k)))]
         peers = [helpers[x][h] for x in range(K) if x != k]
-        n_peer = len(_bits(topo.mask(peers[0], core))) // len(peers)
-        slot = T.ht[:, own * HT * P:(own + 1) * HT * P]
+        n_peer = _share(len(_bits(topo.mask(peers[0], core))), len(peers))
         sent = 0
-        g.wait_ge(sem["hin%d" % own], n_loc)
-        sent += send([(p, slot, slot) for p in peers], sem["hin%d" % own])
-        for part, ysem in ((far[:-1], sem.yfa), (far[-1:], sem.yfb)):
-            for j in part:
-                g.tensor.wait_ge(sem["hin%d" % j], n_loc if j == own else n_peer)
-            g.tensor.wait_ge(ysem, n_loc)
-            for i, r in enumerate(rows):
+        for i in range(len(rows)):
+            g.wait_ge(sem[TSEM[i] % own], n_loc[i])
+            sent += send([(p, ht_ap(own, i), ht_ap(own, i)) for p in peers], sem[TSEM[i] % own])
+        for i, r in enumerate(rows):
+            for part, ysem in ((far[:-1], sem.yfa), (far[-1:], sem.yfb)):
                 for j in part:
-                    o = (j * HT + i) * P
-                    g.tensor.matmul(T["ps%d" % r][:, 0:W], T.ht[:, o:o + P], T.hy[:, j * W:(j + 1) * W],
+                    g.tensor.wait_ge(sem[TSEM[i] % j], n_loc[i] if j == own else n_peer)
+                if i == 0:
+                    g.tensor.wait_ge(ysem, n_fwd)
+                for j in part:
+                    g.tensor.matmul(T["ps%d" % r][:, 0:W], ht_ap(j, i), T.hy[:, j * W:(j + 1) * W],
                                     start=(j == far[0]), stop=(j == far[-1])).then_inc(sem["mm%d" % r], 1)
         for r in rows:
             g.vector.wait_ge(sem["mm%d" % r], len(far))
@@ -145,7 +157,7 @@ def rank_program(g, core, T, topo):
         return sol_a if j in far else sol_b
 
     def top(j):
-        return BOUNDS[0] if j in far else max(BOUND_B, j)
+        return APIECES[0][1] if j in far else max(BOUND_B, j)
 
     def piece_of(r, j):
         if r <= top(j):
@@ -160,7 +172,7 @@ def rank_program(g, core, T, topo):
 
     def eng(j):
         d = dests(j)
-        return len(_bits(topo.mask(cores[j], site(j)[d[0]]))) // len(d)
+        return _share(len(_bits(topo.mask(cores[j], site(j)[d[0]]))), len(d))
 
     s = rank
     sol = site(s)
@@ -198,14 +210,15 @@ def rank_program(g, core, T, topo):
                   for n, k in enumerate(ds)], sem["in%d_0" % s])
     if nl:
         g.wait_ge(sem.ldL, 16)
+
+        def late_ap(r):
+            return T.stage[:, late0 + P * (r - top(s) - 1):late0 + P * (r - top(s))]
+
         if s in far:
             ka = sol.index(core)
-            hp = []
-            for h in range(NH):
-                a = late0 + P * (HROWS[h][0] - top(s) - 1)
-                hp.append((helpers[ka][h], T.stage[:, a:a + HT * P], T.ht[:, s * HT * P:(s + 1) * HT * P]))
-            sent += send(hp, sem["hin%d" % s], within=chip_only(ka))
-            later = [(i, _lo(i), BOUNDS[i]) for i in range(1, NB)]
+            sent += send([(helpers[ka][h], late_ap(HROWS[h][0]), ht_ap(s, 0)) for h in range(NH)],
+                         sem[TSEM[0] % s], first=chip_only(ka))
+            later = [(i, APIECES[i][0] - 1, APIECES[i][1]) for i in range(1, NB)]
         else:
             later = [(1, top(s), N - 1)]
         for i, lo, hi in later:
@@ -213,6 +226,11 @@ def rank_program(g, core, T, topo):
             b = late0 + P * (hi - top(s))
             o = _OFF[s] + W + P * (lo - s)
             sent += send([(sol[k], T.stage[:, a:b], T.land[:, o:o + b - a]) for k in ds], sem["in%d_%d" % (s, i)])
+        if s in far:
+            for h in range(NH):
+                for i in range(1, len(HROWS[h])):
+                    sent += send([(helpers[ka][h], late_ap(HROWS[h][i]), ht_ap(s, i))], sem[TSEM[i] % s],
+                                 only=chip_only(ka))
 
     if solver:
         k = sol.index(core)
@@ -261,13 +279,12 @@ def rank_program(g, core, T, topo):
         order = []
         if at_a:
             for j in range(NA):
-                order += [(r, j) for r in range(j + 1, BOUNDS[0] + 1)]
-            for i in range(1, NB):
-                for r in range(_lo(i) + 1, BOUNDS[i] + 1):
-                    order += [(r, j) for j in range(NA)]
+                order += [(r, j) for r in range(j + 1, NA)]
+            for r in SROWS:
+                order += [(r, j) for j in range(NA)]
         else:
             order += [(r, None) for r in range(NA, N)]
-            first = list(range(NA, BOUNDS[-1] + 1))
+            first = list(EARLY)
             for j in first:
                 order += [(r, j) for r in range(j + 1, BOUND_B + 1)]
             for j in first:
@@ -297,7 +314,7 @@ def rank_program(g, core, T, topo):
         if at_a:
             need_b(g.vector, "v", 0)
             g.vector.tensor_copy(ys_ap(0), b_ap(0)).then_inc(sem.yv0, 1)
-            for r in range(1, BOUNDS[-1] + 1):
+            for r in list(range(1, NA)) + SROWS:
                 if r < NA:
                     need_b(g.vector, "v", r)
                 g.vector.wait_ge(sem["mm%d" % r], total[r])
@@ -310,14 +327,14 @@ def rank_program(g, core, T, topo):
                 for j in range(lo, hi):
                     g.wait_ge(sem["yv%d" % j], 1)
                 sent += send([(helpers[k][h], T.ys[:, lo * W:hi * W], T.hy[:, lo * W:hi * W]) for h in range(NH)],
-                             ysem, within=chip_only(k))
-            for r in range(NA, BOUNDS[-1] + 1):
+                             ysem, first=chip_only(k))
+            for r in SROWS:
                 g.wait_ge(sem["pv%d" % r], 1)
                 sent += send([(sol_b[k], s_ap(r), s_ap(r))], sem["pin%d" % r])
             back = [r for r in range(1, NA) if r != rank]
             sent += send([(cores[r], ys_ap(r), T.yl[:, k * W:(k + 1) * W]) for r in back], sem["res%d" % k])
         else:
-            maker = {r: sol_a[k] for r in range(NA, BOUNDS[-1] + 1)}
+            maker = {r: sol_a[k] for r in SROWS}
             for h in range(NH):
                 for r in HROWS[h]:
                     maker[r] = helpers[k][h]

from concourse.bass import DstId, RemoteDMATransfer
from concourse.mybir import AluOpType

N, P, TK = 9, 128, 512
WORLD = 512
K = 3
W = 176
C0 = [0, 168, 336]
KEEP = [0, 8, 8]
NA = 3
APIECES = [(1, 2), (3, 4)]
NB = len(APIECES)
SROWS = [3, 4]
EARLY = [3, 4]
BOUND_B = 6
HROWS = [[5, 8], [6], [7]]
NH = len(HROWS)
HT = max(len(_x) for _x in HROWS)
TSEM = ["hin%d", "hjn%d"]


def _piece(r):
    return [i for i in range(NB) if APIECES[i][0] <= r <= APIECES[i][1]][0]


_OFF, _c = [], 0
for _s in range(N):
    _OFF.append(_c)
    _c += W + P * (N - 1 - _s)

SCRATCH = {
    "stage": ("sbuf", [P, K * W + P * (N - 1)], "bfloat16"),
    "land": ("sbuf", [P, _c], "bfloat16"),
    "ys": ("sbuf", [P, N * W], "bfloat16"),
    "yl": ("sbuf", [P, K * W], "bfloat16"),
    "psb": ("sbuf", [P, (N - NA) * W], "bfloat16"),
    "ht": ("sbuf", [P, NA * HT * P], "bfloat16"),
    "hy": ("sbuf", [P, NA * W], "bfloat16"),
    "neg1": ("sbuf", [P, P], "bfloat16"),
    "negI": ("sbuf", [P, P], "bfloat16"),
}
for _r in range(1, N):
    SCRATCH["ps%d" % _r] = ("psum", [P, 512], "float32")

SEMAPHORES = (["ldE", "ldL", "ldO", "sent", "yfa", "yfb", "c1", "c2"]
              + ["res%d" % k for k in range(K)] + ["st%d" % k for k in range(K)]
              + ["in%d_%d" % (s, i) for s in range(N) for i in range(NB)]
              + [t % s for s in range(NA) for t in TSEM]
              + ["pv%d" % r for r in range(NA, N)] + ["pin%d" % r for r in range(NA, N)]
              + ["mm%d" % r for r in range(1, N)] + ["yv%d" % r for r in range(N)])


def _bits(mask):
    return [1 << i for i in range(mask.bit_length()) if (mask >> i) & 1]


def _share(n_eng, parts):
    n = 1
    while 2 * n * parts <= n_eng:
        n *= 2
    return n


def _deal(e, parts):
    n = _share(len(e), parts)
    return [sum(e[i * n:(i + 1) * n]) for i in range(parts)]


def rank_program(g, core, T, topo):
    rank = T.rank_of(core)
    cores = list(T.cores)
    sem = T.sem
    hubs = [c for c in cores
            if all(topo.may_write(c, d) and topo.may_write(d, c) for d in cores if d != c)]
    far = [j for j, c in enumerate(cores) if topo.rack(topo.host(c)) != topo.rack(topo.host(hubs[0]))]
    sol_a = [cores[j] for j in far]
    sol_b = [[h for h in hubs if topo.chip(h) == topo.chip(a)][0] for a in sol_a]

    def helpers_of(c):
        mate = [x for x in range(WORLD) if topo.mates(c, x)][0]
        chip = [x for x in range(WORLD) if topo.host(x) == topo.host(c) and topo.chip(x) == topo.chip(c)]
        other = [x for x in chip if topo.die(x) != topo.die(c)]
        same = [x for x in chip if topo.die(x) == topo.die(c)]
        return [[x for x in other if topo.may_write(x, mate)][0], [x for x in other if not topo.may_write(x, mate)][0],
                [x for x in same if topo.may_write(x, mate) != topo.may_write(c, mate)][0]]

    helpers = [helpers_of(c) for c in sol_a]
    role = [(k, h) for k in range(K) for h in range(NH) if helpers[k][h] == core]
    if rank is None and not role:
        return

    def chip_only(k):
        return topo.mask(sol_a[k], helpers[k][0]) & ~topo.mask(sol_a[k], sol_b[k])

    def send(pieces, remote_sem, first=0, only=None):
        common = topo.mask(core, pieces[0][0])
        for d, _a, _b in pieces:
            common &= topo.mask(core, d)
        if only is not None:
            common &= only
        e = [x for x in _bits(common) if x & first] + [x for x in _bits(common) if not x & first]
        if len(pieces) == 1:
            d, src, dst = pieces[0]
            rid, pid = topo.addr(d, core)
            g.remote_dma(dst, src, remote_sem, sem.sent, pid, rid, common)
            return len(_bits(common))
        n = 0
        trs = []
        for (d, src, dst), m in zip(pieces, _deal(e, len(pieces))):
            rid, pid = topo.addr(d, core)
            trs.append(RemoteDMATransfer(dst_ids=[DstId(rid=rid, pnc=pid)], dma_engine_mask=m,
                                         remote_sem=remote_sem, src=src, dst=dst))
            n += len(_bits(m))
        g.remote_dma_fused(trs, local_sem=sem.sent)
        return n

    def s_ap(r):
        return T.psb[:, (r - NA) * W:(r - NA + 1) * W]

    def ht_ap(j, i):
        return T.ht[:, (j * HT + i) * P:(j * HT + i + 1) * P]

    def minus_sum(r):
        g.vector.tensor_scalar(s_ap(r), T["ps%d" % r][:, 0:W], -1.0, None, AluOpType.mult).then_inc(sem["pv%d" % r], 1)

    if role:
        k, h = role[0]
        rows = HROWS[h]
        own = far[k]
        n_fwd = _share(len(_bits(topo.mask(sol_a[k], core))), NH)
        n_loc = [n_fwd, len(_bits(chip_only(k)))]
        peers = [helpers[x][h] for x in range(K) if x != k]
        n_peer = _share(len(_bits(topo.mask(peers[0], core))), len(peers))
        sent = 0
        for i in range(len(rows)):
            g.wait_ge(sem[TSEM[i] % own], n_loc[i])
            sent += send([(p, ht_ap(own, i), ht_ap(own, i)) for p in peers], sem[TSEM[i] % own])
        for i, r in enumerate(rows):
            for part, ysem in ((far[:-1], sem.yfa), (far[-1:], sem.yfb)):
                for j in part:
                    g.tensor.wait_ge(sem[TSEM[i] % j], n_loc[i] if j == own else n_peer)
                if i == 0:
                    g.tensor.wait_ge(ysem, n_fwd)
                for j in part:
                    g.tensor.matmul(T["ps%d" % r][:, 0:W], ht_ap(j, i), T.hy[:, j * W:(j + 1) * W],
                                    start=(j == far[0]), stop=(j == far[-1])).then_inc(sem["mm%d" % r], 1)
        for r in rows:
            g.vector.wait_ge(sem["mm%d" % r], len(far))
            minus_sum(r)
        for r in rows:
            g.wait_ge(sem["pv%d" % r], 1)
            sent += send([(sol_b[k], s_ap(r), s_ap(r))], sem["pin%d" % r])
        g.wait_ge(sem.sent, sent)
        return

    def site(j):
        return sol_a if j in far else sol_b

    def top(j):
        return APIECES[0][1] if j in far else max(BOUND_B, j)

    def piece_of(r, j):
        if r <= top(j):
            return 0
        return _piece(r) if j in far else 1

    def ns_(j):
        return top(j) - j

    def dests(j):
        return [k for k, c in enumerate(site(j)) if c != cores[j]]

    def eng(j):
        d = dests(j)
        return _share(len(_bits(topo.mask(cores[j], site(j)[d[0]]))), len(d))

    s = rank
    sol = site(s)
    ds = dests(s)
    ns = ns_(s)
    nl = N - 1 - top(s)
    w1 = W + P * ns
    runs = [0, W, 2 * W + P * ns][:len(ds)]
    late0 = runs[-1] + w1
    own0 = late0 + P * nl
    solver = core in sol

    nE = 0
    for n, k in enumerate(ds):
        o = runs[n] + (0 if n == 0 else P * ns)
        g.sync.dma_start(T.stage[:, o:o + W], T.b[:, C0[k]:C0[k] + W]).then_inc(sem.ldE, 16)
        nE += 16
    if ns:
        for o in [W] + runs[2:]:
            g.scalar.dma_start(T.stage[:, o:o + P * ns], T.l[:, P * (s + 1):P * (s + 1 + ns)]).then_inc(sem.ldE, 16)
            nE += 16
    if nl:
        g.scalar.dma_start(T.stage[:, late0:late0 + P * nl], T.l[:, P * (N - nl):P * N]).then_inc(sem.ldL, 16)
    if solver:
        kk = sol.index(core)
        g.sync.dma_start(T.stage[:, own0:own0 + W], T.b[:, C0[kk]:C0[kk] + W]).then_inc(sem.ldO, 16)
    if solver and s not in far:
        g.vector.memset(T.neg1[:], -1.0).then_inc(sem.c1, 1)
        g.wait_ge(sem.c1, 1)
        g.affine_select(T.negI[:], T.neg1[:], [[-1, P]], AluOpType.is_equal, 0.0, 0, 1).then_inc(sem.c2, 1)

    sent = 0
    g.wait_ge(sem.ldE, nE)
    sent += send([(sol[k], T.stage[:, runs[n]:runs[n] + w1], T.land[:, _OFF[s]:_OFF[s] + w1])
                  for n, k in enumerate(ds)], sem["in%d_0" % s])
    if nl:
        g.wait_ge(sem.ldL, 16)

        def late_ap(r):
            return T.stage[:, late0 + P * (r - top(s) - 1):late0 + P * (r - top(s))]

        if s in far:
            ka = sol.index(core)
            sent += send([(helpers[ka][h], late_ap(HROWS[h][0]), ht_ap(s, 0)) for h in range(NH)],
                         sem[TSEM[0] % s], first=chip_only(ka))
            later = [(i, APIECES[i][0] - 1, APIECES[i][1]) for i in range(1, NB)]
        else:
            later = [(1, top(s), N - 1)]
        for i, lo, hi in later:
            a = late0 + P * (lo - top(s))
            b = late0 + P * (hi - top(s))
            o = _OFF[s] + W + P * (lo - s)
            sent += send([(sol[k], T.stage[:, a:b], T.land[:, o:o + b - a]) for k in ds], sem["in%d_%d" % (s, i)])
        if s in far:
            for h in range(NH):
                for i in range(1, len(HROWS[h])):
                    sent += send([(helpers[ka][h], late_ap(HROWS[h][i]), ht_ap(s, i))], sem[TSEM[i] % s],
                                 only=chip_only(ka))

    if solver:
        k = sol.index(core)
        at_a = s in far
        waited = {"t": set(), "v": set()}

        def once(q, tag, key, sm, val):
            if key not in waited[tag]:
                waited[tag].add(key)
                q.wait_ge(sm, val)

        def arrives(q, tag, j, i):
            if j == rank:
                if i == 0:
                    once(q, tag, "ldE", sem.ldE, nE)
                else:
                    once(q, tag, "ldL", sem.ldL, 16)
            else:
                once(q, tag, (j, i), sem["in%d_%d" % (j, i)], eng(j))

        def need_b(q, tag, j):
            if j == rank:
                once(q, tag, "ldO", sem.ldO, 16)
            else:
                arrives(q, tag, j, 0)

        def b_ap(j):
            if j == rank:
                return T.stage[:, own0:own0 + W]
            o = _OFF[j] + (0 if dests(j).index(k) == 0 else P * ns_(j))
            return T.land[:, o:o + W]

        def tile_ap(r, j):
            if j == rank:
                o = W + P * (r - j - 1) if r <= top(j) else late0 + P * (r - top(j) - 1)
                return T.stage[:, o:o + P]
            if r > top(j):
                o = _OFF[j] + W + P * (r - j - 1)
            else:
                o = _OFF[j] + (W if dests(j).index(k) == 0 else 0) + P * (r - j - 1)
            return T.land[:, o:o + P]

        def ys_ap(j):
            return T.ys[:, j * W:(j + 1) * W]

        order = []
        if at_a:
            for j in range(NA):
                order += [(r, j) for r in range(j + 1, NA)]
            for r in SROWS:
                order += [(r, j) for j in range(NA)]
        else:
            order += [(r, None) for r in range(NA, N)]
            first = list(EARLY)
            for j in first:
                order += [(r, j) for r in range(j + 1, BOUND_B + 1)]
            for j in first:
                order += [(r, j) for r in range(BOUND_B + 1, N)]
            for j in range(first[-1] + 1, N - 1):
                order += [(r, j) for r in range(j + 1, N)]
        total = {}
        for r, j in order:
            total[r] = total.get(r, 0) + 1
        count = {}
        for r, j in order:
            count[r] = count.get(r, 0) + 1
            if j is None:
                once(g.tensor, "t", "c2", sem.c2, 1)
                need_b(g.tensor, "t", r)
                lhs, rhs = T.negI[:], b_ap(r)
            else:
                arrives(g.tensor, "t", j, piece_of(r, j))
                if j == 0:
                    need_b(g.tensor, "t", 0)
                else:
                    once(g.tensor, "t", ("y", j), sem["yv%d" % j], 1)
                lhs, rhs = tile_ap(r, j), (b_ap(0) if j == 0 else ys_ap(j))
            g.tensor.matmul(T["ps%d" % r][:, 0:W], lhs, rhs,
                            start=(count[r] == 1), stop=(count[r] == total[r])).then_inc(sem["mm%d" % r], 1)

        if at_a:
            need_b(g.vector, "v", 0)
            g.vector.tensor_copy(ys_ap(0), b_ap(0)).then_inc(sem.yv0, 1)
            for r in list(range(1, NA)) + SROWS:
                if r < NA:
                    need_b(g.vector, "v", r)
                g.vector.wait_ge(sem["mm%d" % r], total[r])
                if r < NA:
                    g.vector.tensor_tensor(ys_ap(r), b_ap(r), T["ps%d" % r][:, 0:W],
                                           AluOpType.subtract).then_inc(sem["yv%d" % r], 1)
                else:
                    minus_sum(r)
            for lo, hi, ysem in ((0, NA - 1, sem.yfa), (NA - 1, NA, sem.yfb)):
                for j in range(lo, hi):
                    g.wait_ge(sem["yv%d" % j], 1)
                sent += send([(helpers[k][h], T.ys[:, lo * W:hi * W], T.hy[:, lo * W:hi * W]) for h in range(NH)],
                             ysem, first=chip_only(k))
            for r in SROWS:
                g.wait_ge(sem["pv%d" % r], 1)
                sent += send([(sol_b[k], s_ap(r), s_ap(r))], sem["pin%d" % r])
            back = [r for r in range(1, NA) if r != rank]
            sent += send([(cores[r], ys_ap(r), T.yl[:, k * W:(k + 1) * W]) for r in back], sem["res%d" % k])
        else:
            maker = {r: sol_a[k] for r in SROWS}
            for h in range(NH):
                for r in HROWS[h]:
                    maker[r] = helpers[k][h]
            for r in range(NA, N):
                g.vector.wait_ge(sem["pin%d" % r], len(_bits(topo.mask(maker[r], core))))
                g.vector.wait_ge(sem["mm%d" % r], total[r])
                g.vector.tensor_tensor(ys_ap(r), s_ap(r), T["ps%d" % r][:, 0:W],
                                       AluOpType.subtract).then_inc(sem["yv%d" % r], 1)
            for r in range(NA, N):
                if r == rank:
                    continue
                g.wait_ge(sem["yv%d" % r], 1)
                sent += send([(cores[r], ys_ap(r), T.yl[:, k * W:(k + 1) * W])], sem["res%d" % k])

    if rank == 0:
        g.sync.wait_ge(sem.ldE, nE)
        g.sync.dma_start(T.y[:], T.b[:]).then_inc(sem.st0, 16)
        g.sync.wait_ge(sem.st0, 16)
    else:
        queues = [g.sync, g.scalar, g.sync]
        for k, c in enumerate(sol):
            q = queues[k]
            if c == core:
                q.wait_ge(sem["yv%d" % rank], 1)
                src = T.ys[:, rank * W + KEEP[k]:(rank + 1) * W]
            else:
                m = len(_bits(topo.mask(c, core)))
                if rank in far:
                    m //= len([r for r in range(1, NA) if cores[r] != c])
                q.wait_ge(sem["res%d" % k], m)
                src = T.yl[:, k * W + KEEP[k]:(k + 1) * W]
            q.dma_start(T.y[:, C0[k] + KEEP[k]:C0[k] + W], src).then_inc(sem["st%d" % k], 16)
        for k in range(K):
            queues[k].wait_ge(sem["st%d" % k], 16)

    g.wait_ge(sem.sent, sent)
